import numpy as np
import ml_dtypes


def mxq(x, axis, fmt="e4m3"):
    dtype, down = {"e4m3": (ml_dtypes.float8_e4m3fn, 7), "e5m2": (ml_dtypes.float8_e5m2, 14)}[fmt]
    v = np.moveaxis(np.asarray(x, np.float32).astype(ml_dtypes.bfloat16).astype(np.float64), axis, -1)
    blocks = v.reshape(v.shape[:-1] + (-1, 32))
    amax = np.abs(blocks).max(-1, keepdims=True)
    byte = np.maximum(np.where(amax > 0, np.frexp(amax)[1] - 1 + 127, 0) - down, 1)
    scale = np.exp2(byte - 127.0)
    codes = (blocks / scale).astype(np.float32).astype(dtype).astype(np.float64)
    return np.moveaxis((codes * scale).reshape(v.shape), -1, axis)


WIDE = False


def mx_kscale(k):
    if not WIDE:
        return np.ones(k)
    levels = np.array([10, -10, 5, -5, 0])
    if k % 512:
        return np.exp2(np.random.permutation(np.resize(levels, k // 32))).repeat(32)
    a = np.empty((k // 512, 16))
    for p in range(k // 512):
        a[p, :8] = np.random.permutation(np.resize(levels, 8))
        for g in range(8):
            far = levels[np.abs(levels - a[p, g]) >= 10]
            a[p, g + 8] = far[np.random.randint(len(far))]
    return np.exp2(a.ravel()).repeat(32)


def f64(x):
    return np.asarray(x).astype(np.float64)


def striped(idx):
    return np.tile(idx.reshape(-1, 16).T, (8, 1)).astype(np.uint16)


def unstriped(offs):
    return offs[:16].T.reshape(-1).astype(np.int64)


def pack_weight(w):
    k, n = w.shape
    w = f64(np.asarray(w, np.float32).astype(ml_dtypes.bfloat16)).reshape(k // 32, 32, n)
    amax = np.abs(w).max(1)
    byte = np.clip(np.where(amax > 0, np.frexp(amax)[1] - 1 + 127 - 7, 1), 1, 254)
    scaled = (w * np.exp2(127.0 - byte)[:, None, :]).reshape(k, n).astype(np.float32)
    words = np.ascontiguousarray(scaled.reshape(k // 512, 128, 4, n).transpose(0, 1, 3, 2)).astype(ml_dtypes.float8_e4m3fn).view(np.uint8)
    return words, np.ascontiguousarray(byte.astype(np.uint8).reshape(k // 512, 16, n))


def unpack_weight(words, scales):
    g, p, n, _ = words.shape
    vals = np.ascontiguousarray(words).view(ml_dtypes.float8_e4m3fn).astype(np.float64) * np.repeat(np.exp2(scales.astype(np.float64) - 127.0), 8, axis=1)[..., None]
    return vals.transpose(0, 1, 3, 2).reshape(g * 512, n)


K, T, S, V, D, W = 512, 4096, 1024, 128, 4, 512


def setup_inputs():
    n = np.random.standard_normal
    s = mx_kscale(K)[:, None]
    packed_xT = pack_weight(n((K, T)) * s)
    return {
        "x_words": packed_xT[0],
        "x_scales": packed_xT[1],
        "lc": (n((K, W)) / np.sqrt(K) / s).astype(np.float32),
        "th": (n((K, V)) / np.sqrt(K) / s).astype(np.float32),
        "alpha": (np.random.uniform(0.3, 1.5, (S, 1))).astype(np.float32),
        "offs": striped(np.random.permutation(T)[:S]),
    }


def reference(x_words, x_scales, lc, th, alpha, offs):
    xq = unpack_weight(x_words, x_scales)[:, unstriped(offs)]
    thq = mxq(f64(th), 0, "e4m3")
    y = xq.T @ thq
    lcq = mxq(f64(lc), 0, "e4m3")
    z = xq.T @ lcq
    z2 = (z) ** 2
    bon = np.sqrt(z2.reshape(len(z2), -1, D).sum(axis=2) + 0.05)
    ucb = y + f64(alpha) * bon
    sc = 2.0 * ucb
    ex = np.exp(sc - sc.max(axis=1, keepdims=True))
    return ex / ex.sum(axis=1, keepdims=True)

@@ -1,0 +1,146 @@
+from contextlib import ExitStack
+
+import concourse.mybir as mybir
+
+K, T, S, V, D, W = 512, 4096, 1024, 128, 4, 512
+FLOPS = 2 * K * S * (V + W)
+
+F32 = mybir.dt.float32
+BF16 = mybir.dt.bfloat16
+I32 = mybir.dt.int32
+U32 = mybir.dt.uint32
+U16 = mybir.dt.uint16
+U8 = mybir.dt.uint8
+FP8X4 = mybir.dt.float8_e4m3fn_x4
+ACT = mybir.ActivationFunctionType
+ALU = mybir.AluOpType
+AX = mybir.AxisListType
+
+P = 128
+PACK = 4
+HALF = S // 2
+TILES = S // P
+TPH = TILES // 2
+
+
+def tile_picked_ylucb_soft_p_kernel(tc, x_words, x_scales, lc, th, alpha, offs, out):
+    nc = tc.nc
+    with ExitStack() as ctx:
+        keep = ctx.enter_context(tc.tile_pool(name="keep", bufs=1))
+        zps = ctx.enter_context(tc.psum_pool(name="zps", bufs=6))
+        yps = ctx.enter_context(tc.psum_pool(name="yps", bufs=2))
+
+        offsets = keep.tile([P, S // 16], U16, name="offsets")
+        nc.sync.dma_start(offsets[:], offs)
+
+        sc_table = keep.tile([P, T], U8, name="sc_table", align_bytes=64)
+        nc.sync.dma_start(out=sc_table[P - 16 : P, :].bitcast(I32), in_=x_scales[0].bitcast(I32))
+        nc.vector.memset(sc_table[0 : P - 16, :].bitcast(I32), 0)
+
+        warm = keep.tile([P, 2], F32, name="warm")
+        nc.gpsimd.memset(warm[:, 0:1], 1.0)
+        nc.scalar.activation(out=warm[:, 1:2], in_=warm[:, 0:1], func=ACT.Sqrt)
+
+        lc_raw = keep.tile([P, PACK, W], F32, name="lc_raw")
+        nc.sync.dma_start(out=lc_raw[:], in_=lc.rearrange("(p j) w -> p j w", j=PACK))
+        x_table = keep.tile([P, T], U32, name="x_table", align_bytes=64)
+        nc.sync.dma_start(out=x_table[:].bitcast(I32), in_=x_words[0].rearrange("p n t -> p (n t)").bitcast(I32))
+        th_raw = keep.tile([P, PACK, V], F32, name="th_raw")
+        nc.sync.dma_start(out=th_raw[:], in_=th.rearrange("(p j) w -> p j w", j=PACK))
+        alpha_sb = keep.tile([P, TILES], F32, name="alpha_sb")
+        with nc.allow_non_contiguous_dma(reason="one value a partition and tile"):
+            nc.sync.dma_start(out=alpha_sb[:], in_=alpha.rearrange("(i p) o -> p (i o)", p=P))
+
+        x_plane = keep.tile([P, S], U8, name="x_plane", align_bytes=64)
+        nc.vector.memset(x_plane[:].bitcast(I32), 0)
+        sc_picked = keep.tile([P, S], U8, name="sc_picked", align_bytes=64)
+        nc.vector.tensor_copy(sc_picked[:], sc_table[:].indirect(offsets[:]))
+        for q in range(4):
+            nc.scalar.dma_start(
+                out=x_plane[32 * q : 32 * q + 4, :].bitcast(I32),
+                in_=sc_picked[P - 16 + 4 * q : P - 12 + 4 * q, :].bitcast(I32),
+            )
+
+        lc_bf = keep.tile([P, W * PACK], BF16, name="lc_bf", align_bytes=64)
+        nc.scalar.copy(
+            out=lc_bf[:].rearrange("p (c i j) -> p c j i", i=4, j=PACK),
+            in_=lc_raw[:].rearrange("p j (c i) -> p c j i", i=4),
+        )
+        lc_codes = keep.tile([P, W], U32, name="lc_codes", align_bytes=64)
+        lc_plane = keep.tile([P, W], U8, name="lc_plane", align_bytes=64)
+        nc.vector.quantize_mx(out=lc_codes[:].bitcast(FP8X4), scales=lc_plane[:], in_=lc_bf[:])
+
+        x_picked = []
+        for h in range(2):
+            xp = keep.tile([P, HALF], U32, name=f"x_picked{h}", align_bytes=64)
+            cols = HALF // 16
+            nc.vector.tensor_copy(xp[:], x_table[:].indirect(offsets[:, h * cols : (h + 1) * cols]))
+            x_picked.append(xp)
+
+        th_bf = keep.tile([P, V * PACK], BF16, name="th_bf", align_bytes=64)
+        nc.scalar.copy(
+            out=th_bf[:].rearrange("p (c i j) -> p c j i", i=4, j=PACK),
+            in_=th_raw[:].rearrange("p j (c i) -> p c j i", i=4),
+        )
+        th_codes = keep.tile([P, V], U32, name="th_codes", align_bytes=64)
+        th_plane = keep.tile([P, V], U8, name="th_plane", align_bytes=64)
+        nc.vector.quantize_mx(out=th_codes[:].bitcast(FP8X4), scales=th_plane[:], in_=th_bf[:])
+
+        sums = [keep.tile([P, TPH, V], F32, name=f"sums{h}") for h in range(2)]
+        ucb = [keep.tile([P, TPH, V], F32, name=f"ucb{h}") for h in range(2)]
+        bias = [keep.tile([P, TPH], F32, name=f"bias{h}") for h in range(2)]
+        for h in range(2):
+            sq = keep.tile([P, TPH, D, V], F32, name=f"sq{h}")
+            pair = keep.tile([P, TPH, 2, V], F32, name=f"pair{h}")
+            for i in range(TPH):
+                cols = slice(i * P, (i + 1) * P)
+                pcols = slice(h * HALF + i * P, h * HALF + (i + 1) * P)
+                z = zps.tile([P, W], F32, name="z")
+                nc.tensor.matmul_mx(
+                    out=z[:], lhsT=x_picked[h][:, cols].bitcast(FP8X4), lhsT_scale=x_plane[:, pcols],
+                    rhs=lc_codes[:].bitcast(FP8X4), rhs_scale=lc_plane[:], start=True, stop=True,
+                )
+                nc.scalar.activation(out=sq[:, i, :, :], in_=z[:].rearrange("p (v d) -> p d v", d=D), func=ACT.Square)
+                nc.vector.tensor_tensor(out=pair[:, i, :, :], in0=sq[:, i, 0:2, :], in1=sq[:, i, 2:4, :], op=ALU.add)
+                if i % 2 == 1:
+                    nc.vector.tensor_tensor(
+                        out=sums[h][:, i - 1 : i + 1, :], in0=pair[:, i - 1 : i + 1, 0, :],
+                        in1=pair[:, i - 1 : i + 1, 1, :], op=ALU.add,
+                    )
+            y = yps.tile([P, TPH, V], F32, name="y")
+            for i in range(TPH):
+                cols = slice(i * P, (i + 1) * P)
+                pcols = slice(h * HALF + i * P, h * HALF + (i + 1) * P)
+                nc.tensor.matmul_mx(
+                    out=y[:, i, :], lhsT=x_picked[h][:, cols].bitcast(FP8X4), lhsT_scale=x_plane[:, pcols],
+                    rhs=th_codes[:].bitcast(FP8X4), rhs_scale=th_plane[:], start=True, stop=True,
+                )
+            bon = keep.tile([P, TPH, V], F32, name=f"bon{h}")
+            nc.scalar.activation(out=bon[:], in_=sums[h][:], func=ACT.Sqrt, bias=0.05)
+            for i in range(TPH):
+                t = h * TPH + i
+                nc.vector.scalar_tensor_tensor(
+                    out=ucb[h][:, i, :], in0=bon[:, i, :], scalar=alpha_sb[:, t : t + 1], in1=y[:, i, :],
+                    op0=ALU.mult, op1=ALU.add,
+                )
+            top = keep.tile([P, TPH], F32, name=f"top{h}")
+            nc.vector.tensor_reduce(out=top[:], in_=ucb[h][:], axis=AX.X, op=ALU.max)
+            nc.vector.tensor_scalar(out=bias[h][:], in0=top[:], scalar1=-2.0, scalar2=None, op0=ALU.mult)
+
+        out_v = out.rearrange("(i p) v -> p i v", p=P)
+        for h in range(2):
+            ex = sums[1 - h]
+            total = keep.tile([P, TPH], F32, name=f"total{h}")
+            for i in range(TPH):
+                nc.scalar.activation(
+                    out=ex[:, i, :], in_=ucb[h][:, i, :], func=ACT.Exp, bias=bias[h][:, i : i + 1], scale=2.0,
+                    accum_out=total[:, i : i + 1],
+                )
+            inv = keep.tile([P, TPH], F32, name=f"inv{h}")
+            nc.vector.reciprocal(out=inv[:], in_=total[:])
+            res = keep.tile([P, TPH, V], F32, name=f"res{h}")
+            for i in range(TPH):
+                nc.vector.tensor_scalar(
+                    out=res[:, i, :], in0=ex[:, i, :], scalar1=inv[:, i : i + 1], scalar2=None, op0=ALU.mult
+                )
+            nc.sync.dma_start(out=out_v[:, h * TPH : (h + 1) * TPH, :], in_=res[:])

@@ -1,6 +1,7 @@
 from contextlib import ExitStack
 
 import concourse.mybir as mybir
+from concourse.masks import make_identity
 
 K, T, S, V, D, W = 512, 4096, 1024, 128, 4, 512
 FLOPS = 2 * K * S * (V + W)
@@ -27,15 +28,20 @@ def tile_picked_ylucb_soft_p_kernel(tc, x_words, x_scales, lc, th, alpha, offs, 
     nc = tc.nc
     with ExitStack() as ctx:
         keep = ctx.enter_context(tc.tile_pool(name="keep", bufs=1))
-        zps = ctx.enter_context(tc.psum_pool(name="zps", bufs=6))
+        zps = ctx.enter_context(tc.psum_pool(name="zps", bufs=5))
+        sps = ctx.enter_context(tc.psum_pool(name="sps", bufs=1))
         yps = ctx.enter_context(tc.psum_pool(name="yps", bufs=2))
 
         offsets = keep.tile([P, S // 16], U16, name="offsets")
         nc.sync.dma_start(offsets[:], offs)
 
         sc_table = keep.tile([P, T], U8, name="sc_table", align_bytes=64)
-        nc.sync.dma_start(out=sc_table[P - 16 : P, :].bitcast(I32), in_=x_scales[0].bitcast(I32))
+        nc.scalar.dma_start(out=sc_table[P - 16 : P, :].bitcast(I32), in_=x_scales[0].bitcast(I32))
         nc.vector.memset(sc_table[0 : P - 16, :].bitcast(I32), 0)
+
+        alpha_rows = keep.tile([P, P], F32, name="alpha_rows")
+        nc.scalar.dma_start(out=alpha_rows[P - TILES : P, :], in_=alpha.rearrange("(i p) o -> i (p o)", p=P))
+        nc.gpsimd.memset(alpha_rows[0 : P - TILES, :], 0.0)
 
         warm = keep.tile([P, 2], F32, name="warm")
         nc.gpsimd.memset(warm[:, 0:1], 1.0)
@@ -47,9 +53,6 @@ def tile_picked_ylucb_soft_p_kernel(tc, x_words, x_scales, lc, th, alpha, offs, 
         nc.sync.dma_start(out=x_table[:].bitcast(I32), in_=x_words[0].rearrange("p n t -> p (n t)").bitcast(I32))
         th_raw = keep.tile([P, PACK, V], F32, name="th_raw")
         nc.sync.dma_start(out=th_raw[:], in_=th.rearrange("(p j) w -> p j w", j=PACK))
-        alpha_sb = keep.tile([P, TILES], F32, name="alpha_sb")
-        with nc.allow_non_contiguous_dma(reason="one value a partition and tile"):
-            nc.sync.dma_start(out=alpha_sb[:], in_=alpha.rearrange("(i p) o -> p (i o)", p=P))
 
         x_plane = keep.tile([P, S], U8, name="x_plane", align_bytes=64)
         nc.vector.memset(x_plane[:].bitcast(I32), 0)
@@ -61,14 +64,23 @@ def tile_picked_ylucb_soft_p_kernel(tc, x_words, x_scales, lc, th, alpha, offs, 
                 in_=sc_picked[P - 16 + 4 * q : P - 12 + 4 * q, :].bitcast(I32),
             )
 
-        lc_bf = keep.tile([P, W * PACK], BF16, name="lc_bf", align_bytes=64)
-        nc.scalar.copy(
-            out=lc_bf[:].rearrange("p (c i j) -> p c j i", i=4, j=PACK),
-            in_=lc_raw[:].rearrange("p j (c i) -> p c j i", i=4),
-        )
+        ident = keep.tile([P, P], F32, name="ident")
+        make_identity(nc, ident[:])
+        alpha_t = zps.tile([P, HALF], F32, name="z")
+        nc.tensor.transpose(alpha_t[:, 0:P], alpha_rows[:], ident[:])
+        alpha_sb = keep.tile([P, TILES], F32, name="alpha_sb")
+        nc.scalar.copy(out=alpha_sb[:], in_=alpha_t[:, P - TILES : P])
+
+        lc_bf = keep.tile([P, D, V, PACK], BF16, name="lc_bf", align_bytes=64)
+        lc_dst = lc_bf[:].rearrange("p d v j -> p v d j")
+        lc_src = lc_raw[:].rearrange("p j (v d) -> p v d j", d=D)
+        nc.scalar.copy(out=lc_dst[:, 0 : V // 2], in_=lc_src[:, 0 : V // 2])
+        nc.vector.tensor_copy(out=lc_dst[:, V // 2 : V], in_=lc_src[:, V // 2 : V])
         lc_codes = keep.tile([P, W], U32, name="lc_codes", align_bytes=64)
         lc_plane = keep.tile([P, W], U8, name="lc_plane", align_bytes=64)
-        nc.vector.quantize_mx(out=lc_codes[:].bitcast(FP8X4), scales=lc_plane[:], in_=lc_bf[:])
+        nc.vector.quantize_mx(
+            out=lc_codes[:].bitcast(FP8X4), scales=lc_plane[:], in_=lc_bf[:].rearrange("p d v j -> p (d v j)")
+        )
 
         x_picked = []
         for h in range(2):
@@ -77,50 +89,86 @@ def tile_picked_ylucb_soft_p_kernel(tc, x_words, x_scales, lc, th, alpha, offs, 
             nc.vector.tensor_copy(xp[:], x_table[:].indirect(offsets[:, h * cols : (h + 1) * cols]))
             x_picked.append(xp)
 
-        th_bf = keep.tile([P, V * PACK], BF16, name="th_bf", align_bytes=64)
-        nc.scalar.copy(
-            out=th_bf[:].rearrange("p (c i j) -> p c j i", i=4, j=PACK),
-            in_=th_raw[:].rearrange("p j (c i) -> p c j i", i=4),
-        )
+        th_bf = keep.tile([P, V, PACK], BF16, name="th_bf", align_bytes=64)
+        nc.scalar.copy(out=th_bf[:], in_=th_raw[:].rearrange("p j v -> p v j"))
         th_codes = keep.tile([P, V], U32, name="th_codes", align_bytes=64)
         th_plane = keep.tile([P, V], U8, name="th_plane", align_bytes=64)
-        nc.vector.quantize_mx(out=th_codes[:].bitcast(FP8X4), scales=th_plane[:], in_=th_bf[:])
+        nc.vector.quantize_mx(
+            out=th_codes[:].bitcast(FP8X4), scales=th_plane[:], in_=th_bf[:].rearrange("p v j -> p (v j)")
+        )
 
-        sums = [keep.tile([P, TPH, V], F32, name=f"sums{h}") for h in range(2)]
+        def x_tile(t):
+            h, i = divmod(t, TPH)
+            return x_picked[h][:, i * P : (i + 1) * P].bitcast(FP8X4), x_plane[:, t * P : (t + 1) * P]
+
+        sq_a = [keep.tile([P, HALF], F32, name=f"sq_a{d}") for d in range(D)]
+        for d in range(D):
+            cols = slice(d * V, (d + 1) * V)
+            z = zps.tile([P, HALF], F32, name="z")
+            nc.tensor.matmul_mx(
+                out=z[:], lhsT=lc_codes[:, cols].bitcast(FP8X4), lhsT_scale=lc_plane[:, cols],
+                rhs=x_picked[0][:].bitcast(FP8X4), rhs_scale=x_plane[:, 0:HALF], start=True, stop=True,
+            )
+            if d == D - 1:
+                zc = keep.tile([P, HALF], F32, name="zc")
+                nc.vector.tensor_copy(out=zc[:], in_=z[:])
+                nc.vector.tensor_tensor(out=sq_a[d][:], in0=z[:], in1=zc[:], op=ALU.mult)
+            else:
+                nc.scalar.activation(out=sq_a[d][:], in_=z[:], func=ACT.Square)
+
+        sums_b = keep.tile([P, TPH, V], F32, name="sums_b")
+        sq_b = keep.tile([P, TPH, D * V], F32, name="sq_b")
+        pair = keep.tile([P, TPH, 2 * V], F32, name="pair")
+        for i in range(TPH):
+            codes, plane = x_tile(TPH + i)
+            z = zps.tile([P, W], F32, name="z")
+            nc.tensor.matmul_mx(
+                out=z[:], lhsT=codes, lhsT_scale=plane, rhs=lc_codes[:].bitcast(FP8X4), rhs_scale=lc_plane[:],
+                start=True, stop=True,
+            )
+            nc.scalar.activation(out=sq_b[:, i, :], in_=z[:], func=ACT.Square)
+            nc.vector.tensor_tensor(
+                out=pair[:, i, :], in0=sq_b[:, i, 0 : 2 * V], in1=sq_b[:, i, 2 * V : 4 * V], op=ALU.add
+            )
+            if i % 2 == 1:
+                nc.vector.tensor_tensor(
+                    out=sums_b[:, i - 1 : i + 1, :], in0=pair[:, i - 1 : i + 1, 0:V],
+                    in1=pair[:, i - 1 : i + 1, V : 2 * V], op=ALU.add,
+                )
+
+        sums_a = sps.tile([P, TPH, V], F32, name="sums_a")
+        for d in range(D):
+            for i in range(TPH):
+                nc.tensor.matmul(
+                    out=sums_a[:, i, :], lhsT=sq_a[d][:, i * P : (i + 1) * P], rhs=ident[:], is_transpose=True,
+                    start=(d == 0 and i == 0), stop=(d == D - 1 and i == TPH - 1),
+                )
+
+        ys = []
+        for h in range(2):
+            y = yps.tile([P, TPH, V], F32, name="y")
+            for i in range(TPH):
+                codes, plane = x_tile(h * TPH + i)
+                nc.tensor.matmul_mx(
+                    out=y[:, i, :], lhsT=codes, lhsT_scale=plane, rhs=th_codes[:].bitcast(FP8X4),
+                    rhs_scale=th_plane[:], start=True, stop=True,
+                )
+            ys.append(y)
+
+        bon = [keep.tile([P, TPH, V], F32, name=f"bon{h}") for h in range(2)]
+        nc.scalar.activation(out=bon[0][:], in_=sums_a[:], func=ACT.Sqrt, bias=0.05)
+        for g in range(2):
+            nc.scalar.activation(
+                out=bon[1][:, 2 * g : 2 * g + 2, :], in_=sums_b[:, 2 * g : 2 * g + 2, :], func=ACT.Sqrt, bias=0.05
+            )
+
         ucb = [keep.tile([P, TPH, V], F32, name=f"ucb{h}") for h in range(2)]
         bias = [keep.tile([P, TPH], F32, name=f"bias{h}") for h in range(2)]
         for h in range(2):
-            sq = keep.tile([P, TPH, D, V], F32, name=f"sq{h}")
-            pair = keep.tile([P, TPH, 2, V], F32, name=f"pair{h}")
-            for i in range(TPH):
-                cols = slice(i * P, (i + 1) * P)
-                pcols = slice(h * HALF + i * P, h * HALF + (i + 1) * P)
-                z = zps.tile([P, W], F32, name="z")
-                nc.tensor.matmul_mx(
-                    out=z[:], lhsT=x_picked[h][:, cols].bitcast(FP8X4), lhsT_scale=x_plane[:, pcols],
-                    rhs=lc_codes[:].bitcast(FP8X4), rhs_scale=lc_plane[:], start=True, stop=True,
-                )
-                nc.scalar.activation(out=sq[:, i, :, :], in_=z[:].rearrange("p (v d) -> p d v", d=D), func=ACT.Square)
-                nc.vector.tensor_tensor(out=pair[:, i, :, :], in0=sq[:, i, 0:2, :], in1=sq[:, i, 2:4, :], op=ALU.add)
-                if i % 2 == 1:
-                    nc.vector.tensor_tensor(
-                        out=sums[h][:, i - 1 : i + 1, :], in0=pair[:, i - 1 : i + 1, 0, :],
-                        in1=pair[:, i - 1 : i + 1, 1, :], op=ALU.add,
-                    )
-            y = yps.tile([P, TPH, V], F32, name="y")
-            for i in range(TPH):
-                cols = slice(i * P, (i + 1) * P)
-                pcols = slice(h * HALF + i * P, h * HALF + (i + 1) * P)
-                nc.tensor.matmul_mx(
-                    out=y[:, i, :], lhsT=x_picked[h][:, cols].bitcast(FP8X4), lhsT_scale=x_plane[:, pcols],
-                    rhs=th_codes[:].bitcast(FP8X4), rhs_scale=th_plane[:], start=True, stop=True,
-                )
-            bon = keep.tile([P, TPH, V], F32, name=f"bon{h}")
-            nc.scalar.activation(out=bon[:], in_=sums[h][:], func=ACT.Sqrt, bias=0.05)
             for i in range(TPH):
                 t = h * TPH + i
                 nc.vector.scalar_tensor_tensor(
-                    out=ucb[h][:, i, :], in0=bon[:, i, :], scalar=alpha_sb[:, t : t + 1], in1=y[:, i, :],
+                    out=ucb[h][:, i, :], in0=bon[h][:, i, :], scalar=alpha_sb[:, t : t + 1], in1=ys[h][:, i, :],
                     op0=ALU.mult, op1=ALU.add,
                 )
             top = keep.tile([P, TPH], F32, name=f"top{h}")
@@ -129,18 +177,20 @@ def tile_picked_ylucb_soft_p_kernel(tc, x_words, x_scales, lc, th, alpha, offs, 
 
         out_v = out.rearrange("(i p) v -> p i v", p=P)
         for h in range(2):
-            ex = sums[1 - h]
+            ex = (sums_b if h == 0 else bon[0])
             total = keep.tile([P, TPH], F32, name=f"total{h}")
             for i in range(TPH):
                 nc.scalar.activation(
-                    out=ex[:, i, :], in_=ucb[h][:, i, :], func=ACT.Exp, bias=bias[h][:, i : i + 1], scale=2.0,
-                    accum_out=total[:, i : i + 1],
+                    out=ex[:, TPH - 1 - i, :], in_=ucb[h][:, i, :], func=ACT.Exp, bias=bias[h][:, i : i + 1],
+                    scale=2.0, accum_out=total[:, i : i + 1],
                 )
             inv = keep.tile([P, TPH], F32, name=f"inv{h}")
-            nc.vector.reciprocal(out=inv[:], in_=total[:])
             res = keep.tile([P, TPH, V], F32, name=f"res{h}")
-            for i in range(TPH):
-                nc.vector.tensor_scalar(
-                    out=res[:, i, :], in0=ex[:, i, :], scalar1=inv[:, i : i + 1], scalar2=None, op0=ALU.mult
-                )
-            nc.sync.dma_start(out=out_v[:, h * TPH : (h + 1) * TPH, :], in_=res[:])
+            for lo, hi in ((0, 2), (2, 4)) if h == 0 else ((0, 2), (2, 3), (3, 4)):
+                nc.vector.reciprocal(out=inv[:, lo:hi], in_=total[:, lo:hi])
+                for i in range(lo, hi):
+                    nc.vector.tensor_scalar(
+                        out=res[:, i, :], in0=ex[:, TPH - 1 - i, :], scalar1=inv[:, i : i + 1], scalar2=None,
+                        op0=ALU.mult,
+                    )
+                nc.sync.dma_start(out=out_v[:, h * TPH + lo : h * TPH + hi, :], in_=res[:, lo:hi, :])

@@ -22,25 +22,28 @@ PACK = 4
 HALF = S // 2
 TILES = S // P
 TPH = TILES // 2
+X_CUT = T - 512
+WARM_PASSES = 5
+WARM_N = 256
 
 
 def tile_picked_ylucb_soft_p_kernel(tc, x_words, x_scales, lc, th, alpha, offs, out):
     nc = tc.nc
     with ExitStack() as ctx:
         keep = ctx.enter_context(tc.tile_pool(name="keep", bufs=1))
-        zps = ctx.enter_context(tc.psum_pool(name="zps", bufs=5))
-        sps = ctx.enter_context(tc.psum_pool(name="sps", bufs=1))
-        yps = ctx.enter_context(tc.psum_pool(name="yps", bufs=2))
+        psum = ctx.enter_context(tc.psum_pool(name="psum", bufs=1))
+
+        def bank(b, shape):
+            return psum.tile(shape, F32, name=f"bank{b}", tag=f"bank{b}")
 
         offsets = keep.tile([P, S // 16], U16, name="offsets")
         nc.sync.dma_start(offsets[:], offs)
 
         sc_table = keep.tile([P, T], U8, name="sc_table", align_bytes=64)
-        nc.scalar.dma_start(out=sc_table[P - 16 : P, :].bitcast(I32), in_=x_scales[0].bitcast(I32))
+        nc.sync.dma_start(out=sc_table[P - 16 : P, :].bitcast(I32), in_=x_scales[0].bitcast(I32))
         nc.vector.memset(sc_table[0 : P - 16, :].bitcast(I32), 0)
 
         alpha_rows = keep.tile([P, P], F32, name="alpha_rows")
-        nc.scalar.dma_start(out=alpha_rows[P - TILES : P, :], in_=alpha.rearrange("(i p) o -> i (p o)", p=P))
         nc.gpsimd.memset(alpha_rows[0 : P - TILES, :], 0.0)
 
         warm = keep.tile([P, 2], F32, name="warm")
@@ -50,7 +53,10 @@ def tile_picked_ylucb_soft_p_kernel(tc, x_words, x_scales, lc, th, alpha, offs, 
         lc_raw = keep.tile([P, PACK, W], F32, name="lc_raw")
         nc.sync.dma_start(out=lc_raw[:], in_=lc.rearrange("(p j) w -> p j w", j=PACK))
         x_table = keep.tile([P, T], U32, name="x_table", align_bytes=64)
-        nc.sync.dma_start(out=x_table[:].bitcast(I32), in_=x_words[0].rearrange("p n t -> p (n t)").bitcast(I32))
+        x_src = x_words[0].rearrange("p n t -> p (n t)").bitcast(I32)
+        nc.sync.dma_start(out=x_table[:, 0:X_CUT].bitcast(I32), in_=x_src[:, 0:X_CUT])
+        nc.sync.dma_start(out=alpha_rows[P - TILES : P, :], in_=alpha.rearrange("(i p) o -> i (p o)", p=P))
+        nc.sync.dma_start(out=x_table[:, X_CUT:T].bitcast(I32), in_=x_src[:, X_CUT:T])
         th_raw = keep.tile([P, PACK, V], F32, name="th_raw")
         nc.sync.dma_start(out=th_raw[:], in_=th.rearrange("(p j) w -> p j w", j=PACK))
 
@@ -66,10 +72,6 @@ def tile_picked_ylucb_soft_p_kernel(tc, x_words, x_scales, lc, th, alpha, offs, 
 
         ident = keep.tile([P, P], F32, name="ident")
         make_identity(nc, ident[:])
-        alpha_t = zps.tile([P, HALF], F32, name="z")
-        nc.tensor.transpose(alpha_t[:, 0:P], alpha_rows[:], ident[:])
-        alpha_sb = keep.tile([P, TILES], F32, name="alpha_sb")
-        nc.scalar.copy(out=alpha_sb[:], in_=alpha_t[:, P - TILES : P])
 
         lc_bf = keep.tile([P, D, V, PACK], BF16, name="lc_bf", align_bytes=64)
         lc_dst = lc_bf[:].rearrange("p d v j -> p v d j")
@@ -82,6 +84,16 @@ def tile_picked_ylucb_soft_p_kernel(tc, x_words, x_scales, lc, th, alpha, offs, 
             out=lc_codes[:].bitcast(FP8X4), scales=lc_plane[:], in_=lc_bf[:].rearrange("p d v j -> p (d v j)")
         )
 
+        alpha_t = bank(7, [P, HALF])
+        nc.tensor.transpose(alpha_t[:, 0:P], alpha_rows[:], ident[:])
+        for w in range(WARM_PASSES):
+            nc.tensor.matmul_mx(
+                out=alpha_t[:, HALF - WARM_N : HALF], lhsT=lc_codes[:, 0:P].bitcast(FP8X4), lhsT_scale=lc_plane[:, 0:P],
+                rhs=lc_codes[:, 0:WARM_N].bitcast(FP8X4), rhs_scale=lc_plane[:, 0:WARM_N], start=True, stop=True,
+            )
+        alpha_sb = keep.tile([P, TILES], F32, name="alpha_sb")
+        nc.scalar.activation(out=alpha_sb[:], in_=alpha_t[:, P - TILES : P], func=ACT.Copy, scale=-2.0)
+
         x_picked = []
         for h in range(2):
             xp = keep.tile([P, HALF], U32, name=f"x_picked{h}", align_bytes=64)
@@ -90,7 +102,7 @@ def tile_picked_ylucb_soft_p_kernel(tc, x_words, x_scales, lc, th, alpha, offs, 
             x_picked.append(xp)
 
         th_bf = keep.tile([P, V, PACK], BF16, name="th_bf", align_bytes=64)
-        nc.scalar.copy(out=th_bf[:], in_=th_raw[:].rearrange("p j v -> p v j"))
+        nc.scalar.activation(out=th_bf[:], in_=th_raw[:].rearrange("p j v -> p v j"), func=ACT.Copy, scale=-2.0)
         th_codes = keep.tile([P, V], U32, name="th_codes", align_bytes=64)
         th_plane = keep.tile([P, V], U8, name="th_plane", align_bytes=64)
         nc.vector.quantize_mx(
@@ -104,7 +116,7 @@ def tile_picked_ylucb_soft_p_kernel(tc, x_words, x_scales, lc, th, alpha, offs, 
         sq_a = [keep.tile([P, HALF], F32, name=f"sq_a{d}") for d in range(D)]
         for d in range(D):
             cols = slice(d * V, (d + 1) * V)
-            z = zps.tile([P, HALF], F32, name="z")
+            z = bank(d, [P, HALF])
             nc.tensor.matmul_mx(
                 out=z[:], lhsT=lc_codes[:, cols].bitcast(FP8X4), lhsT_scale=lc_plane[:, cols],
                 rhs=x_picked[0][:].bitcast(FP8X4), rhs_scale=x_plane[:, 0:HALF], start=True, stop=True,
@@ -121,7 +133,7 @@ def tile_picked_ylucb_soft_p_kernel(tc, x_words, x_scales, lc, th, alpha, offs, 
         pair = keep.tile([P, TPH, 2 * V], F32, name="pair")
         for i in range(TPH):
             codes, plane = x_tile(TPH + i)
-            z = zps.tile([P, W], F32, name="z")
+            z = bank((D + i) % 7, [P, W])
             nc.tensor.matmul_mx(
                 out=z[:], lhsT=codes, lhsT_scale=plane, rhs=lc_codes[:].bitcast(FP8X4), rhs_scale=lc_plane[:],
                 start=True, stop=True,
@@ -136,7 +148,7 @@ def tile_picked_ylucb_soft_p_kernel(tc, x_words, x_scales, lc, th, alpha, offs, 
                     in1=pair[:, i - 1 : i + 1, V : 2 * V], op=ALU.add,
                 )
 
-        sums_a = sps.tile([P, TPH, V], F32, name="sums_a")
+        sums_a = bank(7, [P, TPH, V])
         for d in range(D):
             for i in range(TPH):
                 nc.tensor.matmul(
@@ -146,7 +158,7 @@ def tile_picked_ylucb_soft_p_kernel(tc, x_words, x_scales, lc, th, alpha, offs, 
 
         ys = []
         for h in range(2):
-            y = yps.tile([P, TPH, V], F32, name="y")
+            y = bank(5 + h, [P, TPH, V])
             for i in range(TPH):
                 codes, plane = x_tile(h * TPH + i)
                 nc.tensor.matmul_mx(
@@ -171,9 +183,11 @@ def tile_picked_ylucb_soft_p_kernel(tc, x_words, x_scales, lc, th, alpha, offs, 
                     out=ucb[h][:, i, :], in0=bon[h][:, i, :], scalar=alpha_sb[:, t : t + 1], in1=ys[h][:, i, :],
                     op0=ALU.mult, op1=ALU.add,
                 )
-            top = keep.tile([P, TPH], F32, name=f"top{h}")
-            nc.vector.tensor_reduce(out=top[:], in_=ucb[h][:], axis=AX.X, op=ALU.max)
-            nc.vector.tensor_scalar(out=bias[h][:], in0=top[:], scalar1=-2.0, scalar2=None, op0=ALU.mult)
+                if i == TPH - 1 or (h == 1 and i == 1):
+                    lo = 0 if h == 0 else i - 1
+                    nc.vector.tensor_reduce(
+                        out=bias[h][:, lo : i + 1], in_=ucb[h][:, lo : i + 1, :], axis=AX.X, op=ALU.min
+                    )
 
         out_v = out.rearrange("(i p) v -> p i v", p=P)
         for h in range(2):
@@ -182,7 +196,7 @@ def tile_picked_ylucb_soft_p_kernel(tc, x_words, x_scales, lc, th, alpha, offs, 
             for i in range(TPH):
                 nc.scalar.activation(
                     out=ex[:, TPH - 1 - i, :], in_=ucb[h][:, i, :], func=ACT.Exp, bias=bias[h][:, i : i + 1],
-                    scale=2.0, accum_out=total[:, i : i + 1],
+                    scale=-1.0, accum_out=total[:, i : i + 1],
                 )
             inv = keep.tile([P, TPH], F32, name=f"inv{h}")
             res = keep.tile([P, TPH, V], F32, name=f"res{h}")

@@ -22,9 +22,11 @@ PACK = 4
 HALF = S // 2
 TILES = S // P
 TPH = TILES // 2
-X_CUT = T - 512
-WARM_PASSES = 5
-WARM_N = 256
+VH = V // 2
+WH = W // 2
+S_CUT = 26
+WARM_PASSES = 3
+NORM = "VVVVVVSV"
 
 
 def tile_picked_ylucb_soft_p_kernel(tc, x_words, x_scales, lc, th, alpha, offs, out):
@@ -39,172 +41,222 @@ def tile_picked_ylucb_soft_p_kernel(tc, x_words, x_scales, lc, th, alpha, offs, 
         offsets = keep.tile([P, S // 16], U16, name="offsets")
         nc.sync.dma_start(offsets[:], offs)
 
-        sc_table = keep.tile([P, T], U8, name="sc_table", align_bytes=64)
+        sc_table = keep.tile([P, T], U8, name="sc_table", tag="scales_lc1_sq", align_bytes=64)
         nc.sync.dma_start(out=sc_table[P - 16 : P, :].bitcast(I32), in_=x_scales[0].bitcast(I32))
         nc.vector.memset(sc_table[0 : P - 16, :].bitcast(I32), 0)
 
         alpha_rows = keep.tile([P, P], F32, name="alpha_rows")
         nc.gpsimd.memset(alpha_rows[0 : P - TILES, :], 0.0)
+        nc.scalar.dma_start(out=alpha_rows[P - TILES : P, :], in_=alpha.rearrange("(i p) o -> i (p o)", p=P))
 
-        warm = keep.tile([P, 2], F32, name="warm")
-        nc.gpsimd.memset(warm[:, 0:1], 1.0)
-        nc.scalar.activation(out=warm[:, 1:2], in_=warm[:, 0:1], func=ACT.Sqrt)
+        one = keep.tile([P, 2], F32, name="one")
+        nc.gpsimd.memset(one[:, 0:1], 1.0)
+        nc.scalar.activation(out=one[:, 1:2], in_=one[:, 0:1], func=ACT.Sqrt)
+        floor = keep.tile([P, 1], F32, name="floor", tag="floor_bias0")
+        nc.gpsimd.tensor_scalar(out=floor[:], in0=one[:, 0:1], scalar1=0.05, scalar2=0.0, op0=ALU.mult, op1=ALU.add)
+        unit = keep.tile([P, 1], F32, name="unit", tag="unit_sq0")
+        nc.gpsimd.memset(unit[:], 1.0)
+        zero = keep.tile([P, 1], F32, name="zero", tag="zero_bon0")
+        nc.gpsimd.memset(zero[:], 0.0)
 
-        lc_raw = keep.tile([P, PACK, W], F32, name="lc_raw")
-        nc.sync.dma_start(out=lc_raw[:], in_=lc.rearrange("(p j) w -> p j w", j=PACK))
-        x_table = keep.tile([P, T], U32, name="x_table", align_bytes=64)
+        lc_rows = lc.rearrange("(p j) w -> p j w", j=PACK)
+        lc_raw0 = keep.tile([P, PACK, WH], F32, name="lc_raw0", tag="lc0_th")
+        nc.sync.dma_start(out=lc_raw0[:], in_=lc_rows[:, :, 0:WH])
+        x_table = keep.tile([P, T], U32, name="x_table", tag="words_th_sums", align_bytes=64)
         x_src = x_words[0].rearrange("p n t -> p (n t)").bitcast(I32)
-        nc.sync.dma_start(out=x_table[:, 0:X_CUT].bitcast(I32), in_=x_src[:, 0:X_CUT])
-        nc.sync.dma_start(out=alpha_rows[P - TILES : P, :], in_=alpha.rearrange("(i p) o -> i (p o)", p=P))
-        nc.sync.dma_start(out=x_table[:, X_CUT:T].bitcast(I32), in_=x_src[:, X_CUT:T])
-        th_raw = keep.tile([P, PACK, V], F32, name="th_raw")
-        nc.sync.dma_start(out=th_raw[:], in_=th.rearrange("(p j) w -> p j w", j=PACK))
+        nc.sync.dma_start(out=x_table[:].bitcast(I32), in_=x_src)
 
         x_plane = keep.tile([P, S], U8, name="x_plane", align_bytes=64)
         nc.vector.memset(x_plane[:].bitcast(I32), 0)
         sc_picked = keep.tile([P, S], U8, name="sc_picked", align_bytes=64)
         nc.vector.tensor_copy(sc_picked[:], sc_table[:].indirect(offsets[:]))
         for q in range(4):
-            nc.scalar.dma_start(
+            nc.sync.dma_start(
                 out=x_plane[32 * q : 32 * q + 4, :].bitcast(I32),
                 in_=sc_picked[P - 16 + 4 * q : P - 12 + 4 * q, :].bitcast(I32),
             )
+        lc_raw1 = keep.tile([P, PACK, WH], F32, name="lc_raw1", tag="scales_lc1_sq", align_bytes=64)
+        nc.sync.dma_start(out=lc_raw1[:], in_=lc_rows[:, :, WH:W])
 
         ident = keep.tile([P, P], F32, name="ident")
         make_identity(nc, ident[:])
 
-        lc_bf = keep.tile([P, D, V, PACK], BF16, name="lc_bf", align_bytes=64)
-        lc_dst = lc_bf[:].rearrange("p d v j -> p v d j")
-        lc_src = lc_raw[:].rearrange("p j (v d) -> p v d j", d=D)
-        nc.scalar.copy(out=lc_dst[:, 0 : V // 2], in_=lc_src[:, 0 : V // 2])
-        nc.vector.tensor_copy(out=lc_dst[:, V // 2 : V], in_=lc_src[:, V // 2 : V])
-        lc_codes = keep.tile([P, W], U32, name="lc_codes", align_bytes=64)
-        lc_plane = keep.tile([P, W], U8, name="lc_plane", align_bytes=64)
-        nc.vector.quantize_mx(
-            out=lc_codes[:].bitcast(FP8X4), scales=lc_plane[:], in_=lc_bf[:].rearrange("p d v j -> p (d v j)")
-        )
+        by_d_codes = keep.tile([P, D, 2, VH], U32, name="by_d_codes", align_bytes=64)
+        by_d_plane = keep.tile([P, D, 2, VH], U8, name="by_d_plane", align_bytes=64)
 
-        alpha_t = bank(7, [P, HALF])
-        nc.tensor.transpose(alpha_t[:, 0:P], alpha_rows[:], ident[:])
-        for w in range(WARM_PASSES):
-            nc.tensor.matmul_mx(
-                out=alpha_t[:, HALF - WARM_N : HALF], lhsT=lc_codes[:, 0:P].bitcast(FP8X4), lhsT_scale=lc_plane[:, 0:P],
-                rhs=lc_codes[:, 0:WARM_N].bitcast(FP8X4), rhs_scale=lc_plane[:, 0:WARM_N], start=True, stop=True,
+        def cast_views(h, raw):
+            bf = keep.tile([P, D, VH, PACK], BF16, name=f"lc_bf{h}", tag=f"lc_bf{h}", align_bytes=64)
+            return bf, bf[:].rearrange("p d v j -> p v d j"), raw[:].rearrange("p j (v d) -> p v d j", d=D)
+
+        def quantise_half(h, bf):
+            codes = keep.tile([P, WH], U32, name=f"lc_codes{h}", tag=f"lc_codes{h}", align_bytes=64)
+            plane = keep.tile([P, WH], U8, name=f"lc_plane{h}", align_bytes=64)
+            nc.vector.memset(plane[:].bitcast(I32), 0)
+            nc.vector.quantize_mx(
+                out=codes[:].bitcast(FP8X4), scales=plane[:], in_=bf[:].rearrange("p d v j -> p (d v j)")
             )
+            nc.vector.tensor_copy(out=by_d_codes[:, :, h, :], in_=codes[:].rearrange("p (d v) -> p d v", d=D))
+            nc.vector.tensor_copy(
+                out=by_d_plane[:, :, h, :].bitcast(I32), in_=plane[:].rearrange("p (d v) -> p d v", d=D).bitcast(I32)
+            )
+            return codes, plane
+
+        def gather_words(h, tag):
+            xp = keep.tile([P, HALF], U32, name=f"x_picked{h}", tag=tag, align_bytes=64)
+            cols = HALF // 16
+            nc.vector.tensor_copy(xp[:], x_table[:].indirect(offsets[:, h * cols : (h + 1) * cols]))
+            return xp
+
+        bf0, dst, src = cast_views(0, lc_raw0)
+        nc.scalar.copy(out=dst, in_=src)
+        th_raw = keep.tile([P, PACK, V], F32, name="th_raw", tag="lc0_th")
+        nc.sync.dma_start(out=th_raw[:], in_=th.rearrange("(p j) w -> p j w", j=PACK))
+        halves = [quantise_half(0, bf0)]
+
+        alpha_t = bank(7, [P, P])
+        nc.tensor.transpose(alpha_t[:], alpha_rows[:], ident[:])
         alpha_sb = keep.tile([P, TILES], F32, name="alpha_sb")
         nc.scalar.activation(out=alpha_sb[:], in_=alpha_t[:, P - TILES : P], func=ACT.Copy, scale=-2.0)
 
-        x_picked = []
-        for h in range(2):
-            xp = keep.tile([P, HALF], U32, name=f"x_picked{h}", align_bytes=64)
-            cols = HALF // 16
-            nc.vector.tensor_copy(xp[:], x_table[:].indirect(offsets[:, h * cols : (h + 1) * cols]))
-            x_picked.append(xp)
+        scratch = bank(6, [P, WH])
+        for w in range(WARM_PASSES):
+            codes, plane = halves[0]
+            nc.tensor.matmul_mx(
+                out=scratch[:], lhsT=codes[:, 0:P].bitcast(FP8X4), lhsT_scale=plane[:, 0:P],
+                rhs=codes[:].bitcast(FP8X4), rhs_scale=x_plane[:, 0:WH], start=True, stop=True,
+            )
 
-        th_bf = keep.tile([P, V, PACK], BF16, name="th_bf", align_bytes=64)
-        nc.scalar.activation(out=th_bf[:], in_=th_raw[:].rearrange("p j v -> p v j"), func=ACT.Copy, scale=-2.0)
+        x_picked = [gather_words(0, "x_picked0")]
+        bf1, dst, src = cast_views(1, lc_raw1)
+        nc.scalar.activation(out=dst[:, 0:S_CUT], in_=src[:, 0:S_CUT], func=ACT.Copy, scale=unit[:])
+        nc.vector.tensor_copy(out=dst[:, S_CUT:VH], in_=src[:, S_CUT:VH])
+        halves.append(quantise_half(1, bf1))
+        x_picked.append(gather_words(1, "lc_bf1"))
+
+        def x_tile(t):
+            h, i = divmod(t, TPH)
+            return x_picked[h][:, i * P : (i + 1) * P].bitcast(FP8X4), x_plane[:, t * P : (t + 1) * P]
+
+        sq_a = [
+            keep.tile([P, TPH, WH], F32, name="sq_a0", tag="unit_sq0"),
+            keep.tile([P, TPH, WH], F32, name="sq_a1"),
+        ]
+        for h in range(2):
+            codes, plane = halves[h]
+            for g in range(2):
+                z = bank(2 * h + g, [P, 2, WH])
+                for i in range(2):
+                    x_codes, x_scale = x_tile(2 * g + i)
+                    nc.tensor.matmul_mx(
+                        out=z[:, i, :], lhsT=x_codes, lhsT_scale=x_scale,
+                        rhs=codes[:].bitcast(FP8X4), rhs_scale=plane[:], start=True, stop=True,
+                    )
+                nc.scalar.activation(out=sq_a[h][:, 2 * g : 2 * g + 2, :], in_=z[:], func=ACT.Square)
+
+        sq_b = []
+        for g in range(2):
+            tokens = slice(g * WH, (g + 1) * WH)
+            for e in range(2):
+                z = bank(D + 2 * g + e, [P, 2, WH])
+                for j in range(2):
+                    d = 2 * e + j
+                    nc.tensor.matmul_mx(
+                        out=z[:, j, :], lhsT=by_d_codes[:, d].rearrange("p h v -> p (h v)").bitcast(FP8X4),
+                        lhsT_scale=by_d_plane[:, d].rearrange("p h v -> p (h v)"),
+                        rhs=x_picked[1][:, tokens].bitcast(FP8X4),
+                        rhs_scale=x_plane[:, HALF + g * WH : HALF + (g + 1) * WH], start=True, stop=True,
+                    )
+                sq = keep.tile([P, 2, WH], F32, name=f"sq_b{g}{e}")
+                nc.scalar.activation(out=sq[:], in_=z[:], func=ACT.Square, bias=zero[:])
+                sq_b.append(sq)
+
+        th_bf = keep.tile([P, V, PACK], BF16, name="th_bf", tag="lc_codes1", align_bytes=64)
+        nc.vector.tensor_scalar(
+            out=th_bf[:], in0=th_raw[:].rearrange("p j v -> p v j"), scalar1=-2.0, scalar2=None, op0=ALU.mult
+        )
         th_codes = keep.tile([P, V], U32, name="th_codes", align_bytes=64)
         th_plane = keep.tile([P, V], U8, name="th_plane", align_bytes=64)
         nc.vector.quantize_mx(
             out=th_codes[:].bitcast(FP8X4), scales=th_plane[:], in_=th_bf[:].rearrange("p v j -> p (v j)")
         )
 
-        def x_tile(t):
-            h, i = divmod(t, TPH)
-            return x_picked[h][:, i * P : (i + 1) * P].bitcast(FP8X4), x_plane[:, t * P : (t + 1) * P]
-
-        sq_a = [keep.tile([P, HALF], F32, name=f"sq_a{d}") for d in range(D)]
-        for d in range(D):
-            cols = slice(d * V, (d + 1) * V)
-            z = bank(d, [P, HALF])
-            nc.tensor.matmul_mx(
-                out=z[:], lhsT=lc_codes[:, cols].bitcast(FP8X4), lhsT_scale=lc_plane[:, cols],
-                rhs=x_picked[0][:].bitcast(FP8X4), rhs_scale=x_plane[:, 0:HALF], start=True, stop=True,
-            )
-            if d == D - 1:
-                zc = keep.tile([P, HALF], F32, name="zc")
-                nc.vector.tensor_copy(out=zc[:], in_=z[:])
-                nc.vector.tensor_tensor(out=sq_a[d][:], in0=z[:], in1=zc[:], op=ALU.mult)
-            else:
-                nc.scalar.activation(out=sq_a[d][:], in_=z[:], func=ACT.Square)
-
-        sums_b = keep.tile([P, TPH, V], F32, name="sums_b")
-        sq_b = keep.tile([P, TPH, D * V], F32, name="sq_b")
-        pair = keep.tile([P, TPH, 2 * V], F32, name="pair")
-        for i in range(TPH):
-            codes, plane = x_tile(TPH + i)
-            z = bank((D + i) % 7, [P, W])
-            nc.tensor.matmul_mx(
-                out=z[:], lhsT=codes, lhsT_scale=plane, rhs=lc_codes[:].bitcast(FP8X4), rhs_scale=lc_plane[:],
-                start=True, stop=True,
-            )
-            nc.scalar.activation(out=sq_b[:, i, :], in_=z[:], func=ACT.Square)
-            nc.vector.tensor_tensor(
-                out=pair[:, i, :], in0=sq_b[:, i, 0 : 2 * V], in1=sq_b[:, i, 2 * V : 4 * V], op=ALU.add
-            )
-            if i % 2 == 1:
-                nc.vector.tensor_tensor(
-                    out=sums_b[:, i - 1 : i + 1, :], in0=pair[:, i - 1 : i + 1, 0:V],
-                    in1=pair[:, i - 1 : i + 1, V : 2 * V], op=ALU.add,
-                )
-
-        sums_a = bank(7, [P, TPH, V])
-        for d in range(D):
-            for i in range(TPH):
-                nc.tensor.matmul(
-                    out=sums_a[:, i, :], lhsT=sq_a[d][:, i * P : (i + 1) * P], rhs=ident[:], is_transpose=True,
-                    start=(d == 0 and i == 0), stop=(d == D - 1 and i == TPH - 1),
-                )
-
-        ys = []
+        pair = keep.tile([P, 2, TPH, V], F32, name="pair", tag="words_th_sums", align_bytes=64)
         for h in range(2):
-            y = bank(5 + h, [P, TPH, V])
+            nc.vector.tensor_tensor(out=pair[:, h], in0=sq_a[h][:, :, 0:V], in1=sq_a[h][:, :, V : 2 * V], op=ALU.add)
+        sums_a = keep.tile([P, TPH, 2, VH], F32, name="sums_a")
+        nc.vector.tensor_tensor(
+            out=sums_a[:].rearrange("p t h v -> p h t v"), in0=pair[:, :, :, 0:VH], in1=pair[:, :, :, VH:V], op=ALU.add
+        )
+
+        def scores(h, b):
+            y = bank(b, [P, TPH, V])
             for i in range(TPH):
-                codes, plane = x_tile(h * TPH + i)
+                x_codes, x_scale = x_tile(h * TPH + i)
                 nc.tensor.matmul_mx(
-                    out=y[:, i, :], lhsT=codes, lhsT_scale=plane, rhs=th_codes[:].bitcast(FP8X4),
+                    out=y[:, i, :], lhsT=x_codes, lhsT_scale=x_scale, rhs=th_codes[:].bitcast(FP8X4),
                     rhs_scale=th_plane[:], start=True, stop=True,
                 )
-            ys.append(y)
+            return y
 
-        bon = [keep.tile([P, TPH, V], F32, name=f"bon{h}") for h in range(2)]
-        nc.scalar.activation(out=bon[0][:], in_=sums_a[:], func=ACT.Sqrt, bias=0.05)
+        ys = [scores(0, 3)]
+        sums_b = []
         for g in range(2):
-            nc.scalar.activation(
-                out=bon[1][:, 2 * g : 2 * g + 2, :], in_=sums_b[:, 2 * g : 2 * g + 2, :], func=ACT.Sqrt, bias=0.05
-            )
+            acc = bank(g, [P, 2, V])
+            for d in range(D):
+                e, j = divmod(d, 2)
+                for i in range(2):
+                    nc.tensor.matmul(
+                        out=acc[:, i, :], lhsT=sq_b[2 * g + e][:, j, i * P : (i + 1) * P], rhs=ident[:],
+                        is_transpose=True, start=(d == 0 and i == 0), stop=(d == D - 1 and i == 1),
+                    )
+            sums_b.append(acc)
+        ys.append(scores(1, 7))
 
-        ucb = [keep.tile([P, TPH, V], F32, name=f"ucb{h}") for h in range(2)]
-        bias = [keep.tile([P, TPH], F32, name=f"bias{h}") for h in range(2)]
-        for h in range(2):
-            for i in range(TPH):
-                t = h * TPH + i
+        bon = [
+            keep.tile([P, TPH, V], F32, name="bon0", tag="zero_bon0"),
+            keep.tile([P, TPH, V], F32, name="bon1"),
+        ]
+        nc.scalar.activation(out=bon[0][:], in_=sums_a[:].rearrange("p t h v -> p t (h v)"), func=ACT.Sqrt, bias=floor[:])
+        for g in range(2):
+            nc.scalar.activation(out=bon[1][:, 2 * g : 2 * g + 2, :], in_=sums_b[g][:], func=ACT.Sqrt, bias=floor[:])
+
+        ucb = keep.tile([P, TILES, V], F32, name="ucb")
+        bias = [
+            keep.tile([P, TPH], F32, name="bias0", tag="floor_bias0"),
+            keep.tile([P, TPH], F32, name="bias1"),
+        ]
+        for lo, hi in [[0,4],[4,6],[6,8]]:
+            for t in range(lo, hi):
+                h, i = divmod(t, TPH)
                 nc.vector.scalar_tensor_tensor(
-                    out=ucb[h][:, i, :], in0=bon[h][:, i, :], scalar=alpha_sb[:, t : t + 1], in1=ys[h][:, i, :],
+                    out=ucb[:, t, :], in0=bon[h][:, i, :], scalar=alpha_sb[:, t : t + 1], in1=ys[h][:, i, :],
                     op0=ALU.mult, op1=ALU.add,
                 )
-                if i == TPH - 1 or (h == 1 and i == 1):
-                    lo = 0 if h == 0 else i - 1
-                    nc.vector.tensor_reduce(
-                        out=bias[h][:, lo : i + 1], in_=ucb[h][:, lo : i + 1, :], axis=AX.X, op=ALU.min
-                    )
+            h, i = divmod(lo, TPH)
+            nc.vector.tensor_reduce(out=bias[h][:, i : i + hi - lo], in_=ucb[:, lo:hi, :], axis=AX.X, op=ALU.min)
 
         out_v = out.rearrange("(i p) v -> p i v", p=P)
-        for h in range(2):
-            ex = (sums_b if h == 0 else bon[0])
-            total = keep.tile([P, TPH], F32, name=f"total{h}")
-            for i in range(TPH):
+        ex = [keep.tile([P, V], F32, name=f"ex{t}") for t in range(TILES)]
+        res = keep.tile([P, TILES, V], F32, name="res")
+        for lo, hi in [[0,4],[4,6],[6,8]]:
+            total = keep.tile([P, hi - lo], F32, name=f"total{lo}")
+            for t in range(lo, hi):
+                h, i = divmod(t, TPH)
                 nc.scalar.activation(
-                    out=ex[:, TPH - 1 - i, :], in_=ucb[h][:, i, :], func=ACT.Exp, bias=bias[h][:, i : i + 1],
-                    scale=-1.0, accum_out=total[:, i : i + 1],
+                    out=ex[t][:], in_=ucb[:, t, :], func=ACT.Exp, bias=bias[h][:, i : i + 1],
+                    scale=-1.0, accum_out=total[:, t - lo : t - lo + 1],
                 )
-            inv = keep.tile([P, TPH], F32, name=f"inv{h}")
-            res = keep.tile([P, TPH, V], F32, name=f"res{h}")
-            for lo, hi in ((0, 2), (2, 4)) if h == 0 else ((0, 2), (2, 3), (3, 4)):
-                nc.vector.reciprocal(out=inv[:, lo:hi], in_=total[:, lo:hi])
-                for i in range(lo, hi):
-                    nc.vector.tensor_scalar(
-                        out=res[:, i, :], in0=ex[:, TPH - 1 - i, :], scalar1=inv[:, i : i + 1], scalar2=None,
-                        op0=ALU.mult,
+            inv = keep.tile([P, hi - lo], F32, name=f"inv{lo}")
+            nc.vector.reciprocal(out=inv[:], in_=total[:])
+            for t in range(lo, hi):
+                factor = inv[:, t - lo : t - lo + 1]
+                if NORM[t] == "S":
+                    nc.scalar.activation(out=res[:, t, :], in_=ex[t][:], func=ACT.Copy, scale=factor)
+                elif NORM[t] == "G":
+                    nc.gpsimd.tensor_scalar(
+                        out=res[:, t, :], in0=ex[t][:], scalar1=factor, scalar2=0.0, op0=ALU.mult, op1=ALU.add
                     )
-                nc.sync.dma_start(out=out_v[:, h * TPH + lo : h * TPH + hi, :], in_=res[:, lo:hi, :])
+                else:
+                    nc.vector.tensor_scalar(out=res[:, t, :], in0=ex[t][:], scalar1=factor, scalar2=None, op0=ALU.mult)
+        for lo, hi in [[0,2],[2,4],[4,6],[6,7],[7,8]]:
+            nc.sync.dma_start(out=out_v[:, lo:hi, :], in_=res[:, lo:hi, :])

@@ -24,9 +24,8 @@ TILES = S // P
 TPH = TILES // 2
 VH = V // 2
 WH = W // 2
-S_CUT = 26
-WARM_PASSES = 3
-NORM = "VVVVVVSV"
+S_CUT = 22
+NORM = "VVVVVVSS"
 
 
 def tile_picked_ylucb_soft_p_kernel(tc, x_words, x_scales, lc, th, alpha, offs, out):
@@ -86,7 +85,7 @@ def tile_picked_ylucb_soft_p_kernel(tc, x_words, x_scales, lc, th, alpha, offs, 
 
         def cast_views(h, raw):
             bf = keep.tile([P, D, VH, PACK], BF16, name=f"lc_bf{h}", tag=f"lc_bf{h}", align_bytes=64)
-            return bf, bf[:].rearrange("p d v j -> p v d j"), raw[:].rearrange("p j (v d) -> p v d j", d=D)
+            return bf, bf[:].rearrange("p d v j -> p v j d"), raw[:].rearrange("p j (v d) -> p v j d", d=D)
 
         def quantise_half(h, bf):
             codes = keep.tile([P, WH], U32, name=f"lc_codes{h}", tag=f"lc_codes{h}", align_bytes=64)
@@ -117,14 +116,6 @@ def tile_picked_ylucb_soft_p_kernel(tc, x_words, x_scales, lc, th, alpha, offs, 
         nc.tensor.transpose(alpha_t[:], alpha_rows[:], ident[:])
         alpha_sb = keep.tile([P, TILES], F32, name="alpha_sb")
         nc.scalar.activation(out=alpha_sb[:], in_=alpha_t[:, P - TILES : P], func=ACT.Copy, scale=-2.0)
-
-        scratch = bank(6, [P, WH])
-        for w in range(WARM_PASSES):
-            codes, plane = halves[0]
-            nc.tensor.matmul_mx(
-                out=scratch[:], lhsT=codes[:, 0:P].bitcast(FP8X4), lhsT_scale=plane[:, 0:P],
-                rhs=codes[:].bitcast(FP8X4), rhs_scale=x_plane[:, 0:WH], start=True, stop=True,
-            )
 
         x_picked = [gather_words(0, "x_picked0")]
         bf1, dst, src = cast_views(1, lc_raw1)
@@ -225,20 +216,30 @@ def tile_picked_ylucb_soft_p_kernel(tc, x_words, x_scales, lc, th, alpha, offs, 
             keep.tile([P, TPH], F32, name="bias0", tag="floor_bias0"),
             keep.tile([P, TPH], F32, name="bias1"),
         ]
-        for lo, hi in [[0,4],[4,6],[6,8]]:
-            for t in range(lo, hi):
-                h, i = divmod(t, TPH)
-                nc.vector.scalar_tensor_tensor(
-                    out=ucb[:, t, :], in0=bon[h][:, i, :], scalar=alpha_sb[:, t : t + 1], in1=ys[h][:, i, :],
-                    op0=ALU.mult, op1=ALU.add,
-                )
+
+        def score(t):
+            h, i = divmod(t, TPH)
+            nc.vector.scalar_tensor_tensor(
+                out=ucb[:, t, :], in0=bon[h][:, i, :], scalar=alpha_sb[:, t : t + 1], in1=ys[h][:, i, :],
+                op0=ALU.mult, op1=ALU.add,
+            )
+
+        def least(lo, hi):
             h, i = divmod(lo, TPH)
             nc.vector.tensor_reduce(out=bias[h][:, i : i + hi - lo], in_=ucb[:, lo:hi, :], axis=AX.X, op=ALU.min)
+
+        for t in range(6):
+            score(t)
+        least(0, 4)
+        for t in range(6, 8):
+            score(t)
+        least(4, 6)
+        least(6, 8)
 
         out_v = out.rearrange("(i p) v -> p i v", p=P)
         ex = [keep.tile([P, V], F32, name=f"ex{t}") for t in range(TILES)]
         res = keep.tile([P, TILES, V], F32, name="res")
-        for lo, hi in [[0,4],[4,6],[6,8]]:
+        for lo, hi in [[0,2],[2,4],[4,6],[6,7],[7,8]]:
             total = keep.tile([P, hi - lo], F32, name=f"total{lo}")
             for t in range(lo, hi):
                 h, i = divmod(t, TPH)

@@ -25,6 +25,7 @@ TPH = TILES // 2
 VH = V // 2
 WH = W // 2
 S_CUT = 22
+WARM_PASSES = 3
 NORM = "VVVVVVSS"
 
 
@@ -117,12 +118,20 @@ def tile_picked_ylucb_soft_p_kernel(tc, x_words, x_scales, lc, th, alpha, offs, 
         alpha_sb = keep.tile([P, TILES], F32, name="alpha_sb")
         nc.scalar.activation(out=alpha_sb[:], in_=alpha_t[:, P - TILES : P], func=ACT.Copy, scale=-2.0)
 
+        scratch = bank(6, [P, WH])
+        for w in range(WARM_PASSES):
+            codes, plane = halves[0]
+            nc.tensor.matmul_mx(
+                out=scratch[:], lhsT=codes[:, 0:P].bitcast(FP8X4), lhsT_scale=plane[:, 0:P],
+                rhs=codes[:].bitcast(FP8X4), rhs_scale=x_plane[:, 0:WH], start=True, stop=True,
+            )
+
         x_picked = [gather_words(0, "x_picked0")]
         bf1, dst, src = cast_views(1, lc_raw1)
         nc.scalar.activation(out=dst[:, 0:S_CUT], in_=src[:, 0:S_CUT], func=ACT.Copy, scale=unit[:])
         nc.vector.tensor_copy(out=dst[:, S_CUT:VH], in_=src[:, S_CUT:VH])
         halves.append(quantise_half(1, bf1))
-        x_picked.append(gather_words(1, "lc_bf1"))
+        x_picked.append(gather_words(1, "scales_lc1_sq"))
 
         def x_tile(t):
             h, i = divmod(t, TPH)
@@ -134,15 +143,15 @@ def tile_picked_ylucb_soft_p_kernel(tc, x_words, x_scales, lc, th, alpha, offs, 
         ]
         for h in range(2):
             codes, plane = halves[h]
-            for g in range(2):
-                z = bank(2 * h + g, [P, 2, WH])
-                for i in range(2):
-                    x_codes, x_scale = x_tile(2 * g + i)
+            for b, lo, hi in ((7, 0, 1), (0, 1, 2), (1, 2, 4)) if h == 0 else ((2, 0, 2), (3, 2, 4)):
+                z = bank(b, [P, hi - lo, WH])
+                for t in range(lo, hi):
+                    x_codes, x_scale = x_tile(t)
                     nc.tensor.matmul_mx(
-                        out=z[:, i, :], lhsT=x_codes, lhsT_scale=x_scale,
+                        out=z[:, t - lo, :], lhsT=x_codes, lhsT_scale=x_scale,
                         rhs=codes[:].bitcast(FP8X4), rhs_scale=plane[:], start=True, stop=True,
                     )
-                nc.scalar.activation(out=sq_a[h][:, 2 * g : 2 * g + 2, :], in_=z[:], func=ACT.Square)
+                nc.scalar.activation(out=sq_a[h][:, lo:hi, :], in_=z[:], func=ACT.Square)
 
         sq_b = []
         for g in range(2):

@@ -19,14 +19,15 @@ AX = mybir.AxisListType
 
 P = 128
 PACK = 4
+SCALE_ROWS = K // 32
 HALF = S // 2
 TILES = S // P
 TPH = TILES // 2
 VH = V // 2
 WH = W // 2
-S_CUT = 22
+PAIR = 2 * P
+S_CUT = 24
 WARM_PASSES = 3
-NORM = "VVVVVVSS"
 
 
 def tile_picked_ylucb_soft_p_kernel(tc, x_words, x_scales, lc, th, alpha, offs, out):
@@ -41,9 +42,9 @@ def tile_picked_ylucb_soft_p_kernel(tc, x_words, x_scales, lc, th, alpha, offs, 
         offsets = keep.tile([P, S // 16], U16, name="offsets")
         nc.sync.dma_start(offsets[:], offs)
 
-        sc_table = keep.tile([P, T], U8, name="sc_table", tag="scales_lc1_sq", align_bytes=64)
-        nc.sync.dma_start(out=sc_table[P - 16 : P, :].bitcast(I32), in_=x_scales[0].bitcast(I32))
-        nc.vector.memset(sc_table[0 : P - 16, :].bitcast(I32), 0)
+        sc_table = keep.tile([P, T], U8, name="sc_table", tag="scales_lc1_picked1", align_bytes=64)
+        nc.sync.dma_start(out=sc_table[P - SCALE_ROWS : P, :].bitcast(I32), in_=x_scales[0].bitcast(I32))
+        nc.vector.memset(sc_table[0 : P - SCALE_ROWS, :].bitcast(I32), 0)
 
         alpha_rows = keep.tile([P, P], F32, name="alpha_rows")
         nc.gpsimd.memset(alpha_rows[0 : P - TILES, :], 0.0)
@@ -52,30 +53,32 @@ def tile_picked_ylucb_soft_p_kernel(tc, x_words, x_scales, lc, th, alpha, offs, 
         one = keep.tile([P, 2], F32, name="one")
         nc.gpsimd.memset(one[:, 0:1], 1.0)
         nc.scalar.activation(out=one[:, 1:2], in_=one[:, 0:1], func=ACT.Sqrt)
-        floor = keep.tile([P, 1], F32, name="floor", tag="floor_bias0")
+
+        floor = keep.tile([P, 1], F32, name="floor", tag="floor_bias")
         nc.gpsimd.tensor_scalar(out=floor[:], in0=one[:, 0:1], scalar1=0.05, scalar2=0.0, op0=ALU.mult, op1=ALU.add)
         unit = keep.tile([P, 1], F32, name="unit", tag="unit_sq0")
         nc.gpsimd.memset(unit[:], 1.0)
-        zero = keep.tile([P, 1], F32, name="zero", tag="zero_bon0")
-        nc.gpsimd.memset(zero[:], 0.0)
+        zero_early = keep.tile([P, 1], F32, name="zero_early", tag="zero_bon_early")
+        nc.gpsimd.memset(zero_early[:], 0.0)
+        zero_late = keep.tile([P, 1], F32, name="zero_late", tag="zero_bon_late_inv")
+        nc.gpsimd.memset(zero_late[:], 0.0)
 
         lc_rows = lc.rearrange("(p j) w -> p j w", j=PACK)
         lc_raw0 = keep.tile([P, PACK, WH], F32, name="lc_raw0", tag="lc0_th")
         nc.sync.dma_start(out=lc_raw0[:], in_=lc_rows[:, :, 0:WH])
-        x_table = keep.tile([P, T], U32, name="x_table", tag="words_th_sums", align_bytes=64)
-        x_src = x_words[0].rearrange("p n t -> p (n t)").bitcast(I32)
-        nc.sync.dma_start(out=x_table[:].bitcast(I32), in_=x_src)
+        x_table = keep.tile([P, T], U32, name="x_table", tag="words_pair", align_bytes=64)
+        nc.sync.dma_start(out=x_table[:].bitcast(I32), in_=x_words[0].rearrange("p n t -> p (n t)").bitcast(I32))
 
         x_plane = keep.tile([P, S], U8, name="x_plane", align_bytes=64)
         nc.vector.memset(x_plane[:].bitcast(I32), 0)
         sc_picked = keep.tile([P, S], U8, name="sc_picked", align_bytes=64)
         nc.vector.tensor_copy(sc_picked[:], sc_table[:].indirect(offsets[:]))
         for q in range(4):
+            first = P - SCALE_ROWS + 4 * q
             nc.sync.dma_start(
-                out=x_plane[32 * q : 32 * q + 4, :].bitcast(I32),
-                in_=sc_picked[P - 16 + 4 * q : P - 12 + 4 * q, :].bitcast(I32),
+                out=x_plane[32 * q : 32 * q + 4, :].bitcast(I32), in_=sc_picked[first : first + 4, :].bitcast(I32)
             )
-        lc_raw1 = keep.tile([P, PACK, WH], F32, name="lc_raw1", tag="scales_lc1_sq", align_bytes=64)
+        lc_raw1 = keep.tile([P, PACK, WH], F32, name="lc_raw1", tag="scales_lc1_picked1", align_bytes=64)
         nc.sync.dma_start(out=lc_raw1[:], in_=lc_rows[:, :, WH:W])
 
         ident = keep.tile([P, P], F32, name="ident")
@@ -85,7 +88,7 @@ def tile_picked_ylucb_soft_p_kernel(tc, x_words, x_scales, lc, th, alpha, offs, 
         by_d_plane = keep.tile([P, D, 2, VH], U8, name="by_d_plane", align_bytes=64)
 
         def cast_views(h, raw):
-            bf = keep.tile([P, D, VH, PACK], BF16, name=f"lc_bf{h}", tag=f"lc_bf{h}", align_bytes=64)
+            bf = keep.tile([P, D, VH, PACK], BF16, name=f"lc_bf{h}", align_bytes=64)
             return bf, bf[:].rearrange("p d v j -> p v j d"), raw[:].rearrange("p j (v d) -> p v j d", d=D)
 
         def quantise_half(h, bf):
@@ -101,11 +104,11 @@ def tile_picked_ylucb_soft_p_kernel(tc, x_words, x_scales, lc, th, alpha, offs, 
             )
             return codes, plane
 
-        def gather_words(h, tag):
-            xp = keep.tile([P, HALF], U32, name=f"x_picked{h}", tag=tag, align_bytes=64)
+        def gather_words(n, tag):
+            picked = keep.tile([P, HALF], U32, name=f"x_picked{n}", tag=tag, align_bytes=64)
             cols = HALF // 16
-            nc.vector.tensor_copy(xp[:], x_table[:].indirect(offsets[:, h * cols : (h + 1) * cols]))
-            return xp
+            nc.vector.tensor_copy(picked[:], x_table[:].indirect(offsets[:, n * cols : (n + 1) * cols]))
+            return picked
 
         bf0, dst, src = cast_views(0, lc_raw0)
         nc.scalar.copy(out=dst, in_=src)
@@ -119,8 +122,8 @@ def tile_picked_ylucb_soft_p_kernel(tc, x_words, x_scales, lc, th, alpha, offs, 
         nc.scalar.activation(out=alpha_sb[:], in_=alpha_t[:, P - TILES : P], func=ACT.Copy, scale=-2.0)
 
         scratch = bank(6, [P, WH])
+        codes, plane = halves[0]
         for w in range(WARM_PASSES):
-            codes, plane = halves[0]
             nc.tensor.matmul_mx(
                 out=scratch[:], lhsT=codes[:, 0:P].bitcast(FP8X4), lhsT_scale=plane[:, 0:P],
                 rhs=codes[:].bitcast(FP8X4), rhs_scale=x_plane[:, 0:WH], start=True, stop=True,
@@ -131,142 +134,152 @@ def tile_picked_ylucb_soft_p_kernel(tc, x_words, x_scales, lc, th, alpha, offs, 
         nc.scalar.activation(out=dst[:, 0:S_CUT], in_=src[:, 0:S_CUT], func=ACT.Copy, scale=unit[:])
         nc.vector.tensor_copy(out=dst[:, S_CUT:VH], in_=src[:, S_CUT:VH])
         halves.append(quantise_half(1, bf1))
-        x_picked.append(gather_words(1, "scales_lc1_sq"))
+        x_picked.append(gather_words(1, "scales_lc1_picked1"))
 
         def x_tile(t):
-            h, i = divmod(t, TPH)
-            return x_picked[h][:, i * P : (i + 1) * P].bitcast(FP8X4), x_plane[:, t * P : (t + 1) * P]
+            n, i = divmod(t, TPH)
+            return x_picked[n][:, i * P : (i + 1) * P].bitcast(FP8X4), x_plane[:, t * P : (t + 1) * P]
 
         sq_a = [
             keep.tile([P, TPH, WH], F32, name="sq_a0", tag="unit_sq0"),
             keep.tile([P, TPH, WH], F32, name="sq_a1"),
         ]
-        for h in range(2):
+        for h, b, lo, hi in ((0, 7, 0, 1), (0, 0, 1, 2), (0, 1, 2, 4), (1, 2, 0, 2), (1, 3, 2, 4)):
             codes, plane = halves[h]
-            for b, lo, hi in ((7, 0, 1), (0, 1, 2), (1, 2, 4)) if h == 0 else ((2, 0, 2), (3, 2, 4)):
-                z = bank(b, [P, hi - lo, WH])
-                for t in range(lo, hi):
-                    x_codes, x_scale = x_tile(t)
-                    nc.tensor.matmul_mx(
-                        out=z[:, t - lo, :], lhsT=x_codes, lhsT_scale=x_scale,
-                        rhs=codes[:].bitcast(FP8X4), rhs_scale=plane[:], start=True, stop=True,
-                    )
-                nc.scalar.activation(out=sq_a[h][:, lo:hi, :], in_=z[:], func=ACT.Square)
-
-        sq_b = []
-        for g in range(2):
-            tokens = slice(g * WH, (g + 1) * WH)
-            for e in range(2):
-                z = bank(D + 2 * g + e, [P, 2, WH])
-                for j in range(2):
-                    d = 2 * e + j
-                    nc.tensor.matmul_mx(
-                        out=z[:, j, :], lhsT=by_d_codes[:, d].rearrange("p h v -> p (h v)").bitcast(FP8X4),
-                        lhsT_scale=by_d_plane[:, d].rearrange("p h v -> p (h v)"),
-                        rhs=x_picked[1][:, tokens].bitcast(FP8X4),
-                        rhs_scale=x_plane[:, HALF + g * WH : HALF + (g + 1) * WH], start=True, stop=True,
-                    )
-                sq = keep.tile([P, 2, WH], F32, name=f"sq_b{g}{e}")
-                nc.scalar.activation(out=sq[:], in_=z[:], func=ACT.Square, bias=zero[:])
-                sq_b.append(sq)
+            z = bank(b, [P, hi - lo, WH])
+            for t in range(lo, hi):
+                x_codes, x_scale = x_tile(t)
+                nc.tensor.matmul_mx(
+                    out=z[:, t - lo, :], lhsT=x_codes, lhsT_scale=x_scale,
+                    rhs=codes[:].bitcast(FP8X4), rhs_scale=plane[:], start=True, stop=True,
+                )
+            nc.scalar.activation(out=sq_a[h][:, lo:hi, :], in_=z[:], func=ACT.Square)
 
         th_bf = keep.tile([P, V, PACK], BF16, name="th_bf", tag="lc_codes1", align_bytes=64)
         nc.vector.tensor_scalar(
             out=th_bf[:], in0=th_raw[:].rearrange("p j v -> p v j"), scalar1=-2.0, scalar2=None, op0=ALU.mult
         )
+        pair = keep.tile([P, 2, TPH, 2 * VH], F32, name="pair", tag="words_pair", align_bytes=64)
+        sums_a = keep.tile([P, TPH, 2, VH], F32, name="sums_a")
+
+        def add_first(g, h):
+            t = slice(2 * g, 2 * g + 2)
+            nc.vector.tensor_tensor(
+                out=pair[:, h, t, :], in0=sq_a[h][:, t, 0 : 2 * VH], in1=sq_a[h][:, t, 2 * VH : 4 * VH], op=ALU.add
+            )
+
+        def add_second(g):
+            t = slice(2 * g, 2 * g + 2)
+            nc.vector.tensor_tensor(
+                out=sums_a[:, t].rearrange("p t h v -> p h t v"), in0=pair[:, :, t, 0:VH],
+                in1=pair[:, :, t, VH : 2 * VH], op=ALU.add,
+            )
+
+        add_first(0, 0)
         th_codes = keep.tile([P, V], U32, name="th_codes", align_bytes=64)
         th_plane = keep.tile([P, V], U8, name="th_plane", align_bytes=64)
         nc.vector.quantize_mx(
             out=th_codes[:].bitcast(FP8X4), scales=th_plane[:], in_=th_bf[:].rearrange("p v j -> p (v j)")
         )
+        add_first(0, 1)
+        add_first(1, 0)
+        add_second(0)
+        add_first(1, 1)
+        add_second(1)
+        sums_v = sums_a[:].rearrange("p t h v -> p t (h v)")
 
-        pair = keep.tile([P, 2, TPH, V], F32, name="pair", tag="words_th_sums", align_bytes=64)
-        for h in range(2):
-            nc.vector.tensor_tensor(out=pair[:, h], in0=sq_a[h][:, :, 0:V], in1=sq_a[h][:, :, V : 2 * V], op=ALU.add)
-        sums_a = keep.tile([P, TPH, 2, VH], F32, name="sums_a")
-        nc.vector.tensor_tensor(
-            out=sums_a[:].rearrange("p t h v -> p h t v"), in0=pair[:, :, :, 0:VH], in1=pair[:, :, :, VH:V], op=ALU.add
-        )
+        sq_b = {}
 
-        def scores(h, b):
+        def transposed_squares(b, g, ds, nought):
+            z = bank(b, [P, len(ds), PAIR])
+            for j, d in enumerate(ds):
+                nc.tensor.matmul_mx(
+                    out=z[:, j, :], lhsT=by_d_codes[:, d].rearrange("p h v -> p (h v)").bitcast(FP8X4),
+                    lhsT_scale=by_d_plane[:, d].rearrange("p h v -> p (h v)"),
+                    rhs=x_picked[1][:, g * PAIR : (g + 1) * PAIR].bitcast(FP8X4),
+                    rhs_scale=x_plane[:, HALF + g * PAIR : HALF + (g + 1) * PAIR], start=True, stop=True,
+                )
+            sq = keep.tile([P, len(ds), PAIR], F32, name=f"sq_b{b}")
+            nc.scalar.activation(out=sq[:], in_=z[:], func=ACT.Square, bias=nought)
+            for j, d in enumerate(ds):
+                sq_b[g, d] = sq[:, j, :]
+
+        transposed_squares(0, 0, (0,), 0.0)
+        transposed_squares(4, 0, (1,), 0.0)
+        transposed_squares(5, 0, (2, 3), 0.0)
+        transposed_squares(6, 1, (0, 1), zero_early[:])
+        bon_early = keep.tile([P, 2, V], F32, name="bon_early", tag="zero_bon_early")
+        nc.scalar.activation(out=bon_early[:], in_=sums_v[:, 0:2, :], func=ACT.Sqrt, bias=floor[:])
+        transposed_squares(7, 1, (2,), zero_late[:])
+        transposed_squares(2, 1, (3,), 0.0)
+
+        def products_with_th(n, b):
             y = bank(b, [P, TPH, V])
             for i in range(TPH):
-                x_codes, x_scale = x_tile(h * TPH + i)
+                x_codes, x_scale = x_tile(n * TPH + i)
                 nc.tensor.matmul_mx(
                     out=y[:, i, :], lhsT=x_codes, lhsT_scale=x_scale, rhs=th_codes[:].bitcast(FP8X4),
                     rhs_scale=th_plane[:], start=True, stop=True,
                 )
             return y
 
-        ys = [scores(0, 3)]
+        ys = [products_with_th(0, 3)]
         sums_b = []
         for g in range(2):
             acc = bank(g, [P, 2, V])
             for d in range(D):
-                e, j = divmod(d, 2)
                 for i in range(2):
                     nc.tensor.matmul(
-                        out=acc[:, i, :], lhsT=sq_b[2 * g + e][:, j, i * P : (i + 1) * P], rhs=ident[:],
+                        out=acc[:, i, :], lhsT=sq_b[g, d][:, i * P : (i + 1) * P], rhs=ident[:],
                         is_transpose=True, start=(d == 0 and i == 0), stop=(d == D - 1 and i == 1),
                     )
             sums_b.append(acc)
-        ys.append(scores(1, 7))
+        ys.append(products_with_th(1, 7))
 
-        bon = [
-            keep.tile([P, TPH, V], F32, name="bon0", tag="zero_bon0"),
-            keep.tile([P, TPH, V], F32, name="bon1"),
-        ]
-        nc.scalar.activation(out=bon[0][:], in_=sums_a[:].rearrange("p t h v -> p t (h v)"), func=ACT.Sqrt, bias=floor[:])
-        for g in range(2):
-            nc.scalar.activation(out=bon[1][:, 2 * g : 2 * g + 2, :], in_=sums_b[g][:], func=ACT.Sqrt, bias=floor[:])
+        bon_late = keep.tile([P, TILES - 2, V], F32, name="bon_late", tag="zero_bon_late_inv")
+        for g, sums in enumerate((sums_v[:, 2:4, :], sums_b[0][:], sums_b[1][:])):
+            nc.scalar.activation(out=bon_late[:, 2 * g : 2 * g + 2, :], in_=sums, func=ACT.Sqrt, bias=floor[:])
 
-        ucb = keep.tile([P, TILES, V], F32, name="ucb")
-        bias = [
-            keep.tile([P, TPH], F32, name="bias0", tag="floor_bias0"),
-            keep.tile([P, TPH], F32, name="bias1"),
-        ]
+        neg = keep.tile([P, TILES, V], F32, name="neg")
+        bias = keep.tile([P, TILES], F32, name="bias", tag="floor_bias")
 
-        def score(t):
-            h, i = divmod(t, TPH)
-            nc.vector.scalar_tensor_tensor(
-                out=ucb[:, t, :], in0=bon[h][:, i, :], scalar=alpha_sb[:, t : t + 1], in1=ys[h][:, i, :],
-                op0=ALU.mult, op1=ALU.add,
+        def score(g):
+            for t in (2 * g, 2 * g + 1):
+                n, i = divmod(t, TPH)
+                bon = bon_early[:, t, :] if g == 0 else bon_late[:, t - 2, :]
+                nc.vector.scalar_tensor_tensor(
+                    out=neg[:, t, :], in0=bon, scalar=alpha_sb[:, t : t + 1], in1=ys[n][:, i, :],
+                    op0=ALU.mult, op1=ALU.add,
+                )
+
+        def least(g):
+            t = slice(2 * g, 2 * g + 2)
+            nc.vector.tensor_reduce(out=bias[:, t], in_=neg[:, t, :], axis=AX.X, op=ALU.min)
+
+        pairs = TILES // 2
+        score(0)
+        for g in range(1, pairs):
+            score(g)
+            least(g - 1)
+        least(pairs - 1)
+
+        ex = keep.tile([P, TILES, V], F32, name="ex")
+        inv = keep.tile([P, TILES], F32, name="inv", tag="zero_bon_late_inv")
+        res = keep.tile([P, TILES, V], F32, name="res")
+        for t in range(TILES):
+            total = keep.tile([P, 1], F32, name=f"total{t}")
+            nc.scalar.activation(
+                out=ex[:, t, :], in_=neg[:, t, :], func=ACT.Exp, bias=bias[:, t : t + 1], scale=-1.0,
+                accum_out=total[:],
             )
-
-        def least(lo, hi):
-            h, i = divmod(lo, TPH)
-            nc.vector.tensor_reduce(out=bias[h][:, i : i + hi - lo], in_=ucb[:, lo:hi, :], axis=AX.X, op=ALU.min)
-
-        for t in range(6):
-            score(t)
-        least(0, 4)
-        for t in range(6, 8):
-            score(t)
-        least(4, 6)
-        least(6, 8)
+            nc.vector.reciprocal(out=inv[:, t : t + 1], in_=total[:])
+            if t > 0:
+                nc.vector.tensor_scalar(
+                    out=res[:, t - 1, :], in0=ex[:, t - 1, :], scalar1=inv[:, t - 1 : t], scalar2=None, op0=ALU.mult
+                )
+        last = TILES - 1
+        nc.scalar.activation(out=res[:, last, :], in_=ex[:, last, :], func=ACT.Copy, scale=inv[:, last : last + 1])
 
         out_v = out.rearrange("(i p) v -> p i v", p=P)
-        ex = [keep.tile([P, V], F32, name=f"ex{t}") for t in range(TILES)]
-        res = keep.tile([P, TILES, V], F32, name="res")
-        for lo, hi in [[0,2],[2,4],[4,6],[6,7],[7,8]]:
-            total = keep.tile([P, hi - lo], F32, name=f"total{lo}")
-            for t in range(lo, hi):
-                h, i = divmod(t, TPH)
-                nc.scalar.activation(
-                    out=ex[t][:], in_=ucb[:, t, :], func=ACT.Exp, bias=bias[h][:, i : i + 1],
-                    scale=-1.0, accum_out=total[:, t - lo : t - lo + 1],
-                )
-            inv = keep.tile([P, hi - lo], F32, name=f"inv{lo}")
-            nc.vector.reciprocal(out=inv[:], in_=total[:])
-            for t in range(lo, hi):
-                factor = inv[:, t - lo : t - lo + 1]
-                if NORM[t] == "S":
-                    nc.scalar.activation(out=res[:, t, :], in_=ex[t][:], func=ACT.Copy, scale=factor)
-                elif NORM[t] == "G":
-                    nc.gpsimd.tensor_scalar(
-                        out=res[:, t, :], in0=ex[t][:], scalar1=factor, scalar2=0.0, op0=ALU.mult, op1=ALU.add
-                    )
-                else:
-                    nc.vector.tensor_scalar(out=res[:, t, :], in0=ex[t][:], scalar1=factor, scalar2=None, op0=ALU.mult)
-        for lo, hi in [[0,2],[2,4],[4,6],[6,7],[7,8]]:
+        for lo, hi in ((0, 2), (2, 4), (4, 6), (6, 7), (7, 8)):
             nc.sync.dma_start(out=out_v[:, lo:hi, :], in_=res[:, lo:hi, :])

@@ -26,7 +26,7 @@ TPH = TILES // 2
 VH = V // 2
 WH = W // 2
 PAIR = 2 * P
-S_CUT = 24
+S_CUT = 32
 WARM_PASSES = 3
 
 
@@ -34,6 +34,7 @@ def tile_picked_ylucb_soft_p_kernel(tc, x_words, x_scales, lc, th, alpha, offs, 
     nc = tc.nc
     with ExitStack() as ctx:
         keep = ctx.enter_context(tc.tile_pool(name="keep", bufs=1))
+        placed = ctx.enter_context(tc.tile_pool(name="placed", bufs=1))
         psum = ctx.enter_context(tc.psum_pool(name="psum", bufs=1))
 
         def bank(b, shape):
@@ -42,7 +43,7 @@ def tile_picked_ylucb_soft_p_kernel(tc, x_words, x_scales, lc, th, alpha, offs, 
         offsets = keep.tile([P, S // 16], U16, name="offsets")
         nc.sync.dma_start(offsets[:], offs)
 
-        sc_table = keep.tile([P, T], U8, name="sc_table", tag="scales_lc1_picked1", align_bytes=64)
+        sc_table = placed.tile([P, T], U8, name="sc_table", offset=0, align_bytes=64)
         nc.sync.dma_start(out=sc_table[P - SCALE_ROWS : P, :].bitcast(I32), in_=x_scales[0].bitcast(I32))
         nc.vector.memset(sc_table[0 : P - SCALE_ROWS, :].bitcast(I32), 0)
 
@@ -58,8 +59,6 @@ def tile_picked_ylucb_soft_p_kernel(tc, x_words, x_scales, lc, th, alpha, offs, 
         nc.gpsimd.tensor_scalar(out=floor[:], in0=one[:, 0:1], scalar1=0.05, scalar2=0.0, op0=ALU.mult, op1=ALU.add)
         unit = keep.tile([P, 1], F32, name="unit", tag="unit_sq0")
         nc.gpsimd.memset(unit[:], 1.0)
-        zero_early = keep.tile([P, 1], F32, name="zero_early", tag="zero_bon_early")
-        nc.gpsimd.memset(zero_early[:], 0.0)
         zero_late = keep.tile([P, 1], F32, name="zero_late", tag="zero_bon_late_inv")
         nc.gpsimd.memset(zero_late[:], 0.0)
 
@@ -78,8 +77,11 @@ def tile_picked_ylucb_soft_p_kernel(tc, x_words, x_scales, lc, th, alpha, offs, 
             nc.sync.dma_start(
                 out=x_plane[32 * q : 32 * q + 4, :].bitcast(I32), in_=sc_picked[first : first + 4, :].bitcast(I32)
             )
-        lc_raw1 = keep.tile([P, PACK, WH], F32, name="lc_raw1", tag="scales_lc1_picked1", align_bytes=64)
-        nc.sync.dma_start(out=lc_raw1[:], in_=lc_rows[:, :, WH:W])
+        lc_raw1 = []
+        for n in range(2):
+            raw = placed.tile([P, PACK, WH // 2], F32, name=f"lc_raw1{n}", offset=2048 * n, align_bytes=64)
+            nc.sync.dma_start(out=raw[:], in_=lc_rows[:, :, WH + n * WH // 2 : WH + (n + 1) * WH // 2])
+            lc_raw1.append(raw)
 
         ident = keep.tile([P, P], F32, name="ident")
         make_identity(nc, ident[:])
@@ -88,7 +90,7 @@ def tile_picked_ylucb_soft_p_kernel(tc, x_words, x_scales, lc, th, alpha, offs, 
         by_d_plane = keep.tile([P, D, 2, VH], U8, name="by_d_plane", align_bytes=64)
 
         def cast_views(h, raw):
-            bf = keep.tile([P, D, VH, PACK], BF16, name=f"lc_bf{h}", align_bytes=64)
+            bf = keep.tile([P, D, VH, PACK], BF16, name=f"lc_bf{h}", tag=f"lc_bf{h}", align_bytes=64)
             return bf, bf[:].rearrange("p d v j -> p v j d"), raw[:].rearrange("p j (v d) -> p v j d", d=D)
 
         def quantise_half(h, bf):
@@ -104,8 +106,8 @@ def tile_picked_ylucb_soft_p_kernel(tc, x_words, x_scales, lc, th, alpha, offs, 
             )
             return codes, plane
 
-        def gather_words(n, tag):
-            picked = keep.tile([P, HALF], U32, name=f"x_picked{n}", tag=tag, align_bytes=64)
+        def gather_words(n):
+            picked = keep.tile([P, HALF], U32, name=f"x_picked{n}", align_bytes=64)
             cols = HALF // 16
             nc.vector.tensor_copy(picked[:], x_table[:].indirect(offsets[:, n * cols : (n + 1) * cols]))
             return picked
@@ -129,12 +131,13 @@ def tile_picked_ylucb_soft_p_kernel(tc, x_words, x_scales, lc, th, alpha, offs, 
                 rhs=codes[:].bitcast(FP8X4), rhs_scale=x_plane[:, 0:WH], start=True, stop=True,
             )
 
-        x_picked = [gather_words(0, "x_picked0")]
-        bf1, dst, src = cast_views(1, lc_raw1)
-        nc.scalar.activation(out=dst[:, 0:S_CUT], in_=src[:, 0:S_CUT], func=ACT.Copy, scale=unit[:])
-        nc.vector.tensor_copy(out=dst[:, S_CUT:VH], in_=src[:, S_CUT:VH])
+        x_picked = [gather_words(0), gather_words(1)]
+        bf1, dst, src = cast_views(1, lc_raw1[0])
+        nc.scalar.copy(out=dst[:, 0:S_CUT], in_=src)
+        nc.scalar.activation(
+            out=dst[:, S_CUT:VH], in_=lc_raw1[1][:].rearrange("p j (v d) -> p v j d", d=D), func=ACT.Copy, scale=unit[:]
+        )
         halves.append(quantise_half(1, bf1))
-        x_picked.append(gather_words(1, "scales_lc1_picked1"))
 
         def x_tile(t):
             n, i = divmod(t, TPH)
@@ -142,9 +145,10 @@ def tile_picked_ylucb_soft_p_kernel(tc, x_words, x_scales, lc, th, alpha, offs, 
 
         sq_a = [
             keep.tile([P, TPH, WH], F32, name="sq_a0", tag="unit_sq0"),
-            keep.tile([P, TPH, WH], F32, name="sq_a1"),
+            keep.tile([P, 2, WH], F32, name="sq_a1"),
         ]
-        for h, b, lo, hi in ((0, 7, 0, 1), (0, 0, 1, 2), (0, 1, 2, 4), (1, 2, 0, 2), (1, 3, 2, 4)):
+
+        def direct_squares(h, b, lo, hi):
             codes, plane = halves[h]
             z = bank(b, [P, hi - lo, WH])
             for t in range(lo, hi):
@@ -153,19 +157,23 @@ def tile_picked_ylucb_soft_p_kernel(tc, x_words, x_scales, lc, th, alpha, offs, 
                     out=z[:, t - lo, :], lhsT=x_codes, lhsT_scale=x_scale,
                     rhs=codes[:].bitcast(FP8X4), rhs_scale=plane[:], start=True, stop=True,
                 )
-            nc.scalar.activation(out=sq_a[h][:, lo:hi, :], in_=z[:], func=ACT.Square)
+            return z
 
-        th_bf = keep.tile([P, V, PACK], BF16, name="th_bf", tag="lc_codes1", align_bytes=64)
+        for h, b, lo, hi in ((0, 7, 0, 1), (0, 0, 1, 2), (0, 1, 2, 4), (1, 2, 0, 2)):
+            nc.scalar.activation(out=sq_a[h][:, lo:hi, :], in_=direct_squares(h, b, lo, hi)[:], func=ACT.Square)
+        z_last = direct_squares(1, 3, 2, 4)
+
+        th_bf = keep.tile([P, V, PACK], BF16, name="th_bf", tag="lc_bf1", align_bytes=64)
         nc.vector.tensor_scalar(
             out=th_bf[:], in0=th_raw[:].rearrange("p j v -> p v j"), scalar1=-2.0, scalar2=None, op0=ALU.mult
         )
         pair = keep.tile([P, 2, TPH, 2 * VH], F32, name="pair", tag="words_pair", align_bytes=64)
         sums_a = keep.tile([P, TPH, 2, VH], F32, name="sums_a")
 
-        def add_first(g, h):
+        def add_first(g, h, sq):
             t = slice(2 * g, 2 * g + 2)
             nc.vector.tensor_tensor(
-                out=pair[:, h, t, :], in0=sq_a[h][:, t, 0 : 2 * VH], in1=sq_a[h][:, t, 2 * VH : 4 * VH], op=ALU.add
+                out=pair[:, h, t, :], in0=sq[:, :, 0 : 2 * VH], in1=sq[:, :, 2 * VH : 4 * VH], op=ALU.add
             )
 
         def add_second(g):
@@ -175,22 +183,14 @@ def tile_picked_ylucb_soft_p_kernel(tc, x_words, x_scales, lc, th, alpha, offs, 
                 in1=pair[:, :, t, VH : 2 * VH], op=ALU.add,
             )
 
-        add_first(0, 0)
         th_codes = keep.tile([P, V], U32, name="th_codes", align_bytes=64)
         th_plane = keep.tile([P, V], U8, name="th_plane", align_bytes=64)
         nc.vector.quantize_mx(
             out=th_codes[:].bitcast(FP8X4), scales=th_plane[:], in_=th_bf[:].rearrange("p v j -> p (v j)")
         )
-        add_first(0, 1)
-        add_first(1, 0)
-        add_second(0)
-        add_first(1, 1)
-        add_second(1)
-        sums_v = sums_a[:].rearrange("p t h v -> p t (h v)")
-
         sq_b = {}
 
-        def transposed_squares(b, g, ds, nought):
+        def transposed_products(b, g, ds):
             z = bank(b, [P, len(ds), PAIR])
             for j, d in enumerate(ds):
                 nc.tensor.matmul_mx(
@@ -199,19 +199,14 @@ def tile_picked_ylucb_soft_p_kernel(tc, x_words, x_scales, lc, th, alpha, offs, 
                     rhs=x_picked[1][:, g * PAIR : (g + 1) * PAIR].bitcast(FP8X4),
                     rhs_scale=x_plane[:, HALF + g * PAIR : HALF + (g + 1) * PAIR], start=True, stop=True,
                 )
-            sq = keep.tile([P, len(ds), PAIR], F32, name=f"sq_b{b}")
-            nc.scalar.activation(out=sq[:], in_=z[:], func=ACT.Square, bias=nought)
+            sq = keep.tile([P, len(ds), PAIR], F32, name=f"sq_b{g}{ds[0]}")
             for j, d in enumerate(ds):
                 sq_b[g, d] = sq[:, j, :]
+            return z, sq
 
-        transposed_squares(0, 0, (0,), 0.0)
-        transposed_squares(4, 0, (1,), 0.0)
-        transposed_squares(5, 0, (2, 3), 0.0)
-        transposed_squares(6, 1, (0, 1), zero_early[:])
-        bon_early = keep.tile([P, 2, V], F32, name="bon_early", tag="zero_bon_early")
-        nc.scalar.activation(out=bon_early[:], in_=sums_v[:, 0:2, :], func=ACT.Sqrt, bias=floor[:])
-        transposed_squares(7, 1, (2,), zero_late[:])
-        transposed_squares(2, 1, (3,), 0.0)
+        def transposed_squares(b, g, ds, nought):
+            z, sq = transposed_products(b, g, ds)
+            nc.scalar.activation(out=sq[:], in_=z[:], func=ACT.Square, bias=nought)
 
         def products_with_th(n, b):
             y = bank(b, [P, TPH, V])
@@ -223,22 +218,38 @@ def tile_picked_ylucb_soft_p_kernel(tc, x_words, x_scales, lc, th, alpha, offs, 
                 )
             return y
 
-        ys = [products_with_th(0, 3)]
-        sums_b = []
-        for g in range(2):
-            acc = bank(g, [P, 2, V])
-            for d in range(D):
-                for i in range(2):
-                    nc.tensor.matmul(
-                        out=acc[:, i, :], lhsT=sq_b[g, d][:, i * P : (i + 1) * P], rhs=ident[:],
-                        is_transpose=True, start=(d == 0 and i == 0), stop=(d == D - 1 and i == 1),
-                    )
-            sums_b.append(acc)
-        ys.append(products_with_th(1, 7))
+        z_sb = keep.tile([P, 2, WH], F32, name="z_sb")
+        sq_last = keep.tile([P, 2, WH], F32, name="sq_last")
+        nc.vector.tensor_copy(out=z_sb[:], in_=z_last[:])
+        add_first(0, 0, sq_a[0][:, 0:2, :])
+        nc.vector.tensor_tensor(out=sq_last[:], in0=z_last[:], in1=z_sb[:], op=ALU.mult)
+        add_first(1, 0, sq_a[0][:, 2:4, :])
+        add_first(0, 1, sq_a[1][:])
+        transposed_squares(4, 0, (0, 1), 0.0)
+        transposed_squares(5, 0, (2, 3), 0.0)
+        transposed_squares(6, 1, (0, 1), 0.0)
+        ys = [products_with_th(0, 7), products_with_th(1, 0)]
+        z, sq = transposed_products(4, 1, (2, 3))
+        nc.scalar.activation(out=sq[:, 0, :], in_=z[:, 0, :], func=ACT.Square, bias=zero_late[:])
+        nc.scalar.activation(out=sq[:, 1, :], in_=z[:, 1, :], func=ACT.Square)
+        add_first(1, 1, sq_last[:])
+        add_second(0)
+        add_second(1)
+        sums_v = sums_a[:].rearrange("p t h v -> p t (h v)")
 
-        bon_late = keep.tile([P, TILES - 2, V], F32, name="bon_late", tag="zero_bon_late_inv")
-        for g, sums in enumerate((sums_v[:, 2:4, :], sums_b[0][:], sums_b[1][:])):
-            nc.scalar.activation(out=bon_late[:, 2 * g : 2 * g + 2, :], in_=sums, func=ACT.Sqrt, bias=floor[:])
+        sums_b = [bank(1 + g, [P, 2, V]) for g in range(2)]
+        for g, d in [(g, d) for g in range(2) for d in range(D)]:
+            for i in range(2):
+                nc.tensor.matmul(
+                    out=sums_b[g][:, i, :], lhsT=sq_b[g, d][:, i * P : (i + 1) * P], rhs=ident[:],
+                    is_transpose=True, start=(d == 0 and i == 0), stop=(d == D - 1 and i == 1),
+                )
+
+        bon = keep.tile([P, TILES, V], F32, name="bon", tag="zero_bon_late_inv")
+        sums = (sums_v[:, 0:2, :], sums_v[:, 2:4, :], sums_b[0][:], sums_b[1][:])
+        order = (2, 0, 1, 3)
+        for g in order:
+            nc.scalar.activation(out=bon[:, 2 * g : 2 * g + 2, :], in_=sums[g], func=ACT.Sqrt, bias=floor[:])
 
         neg = keep.tile([P, TILES, V], F32, name="neg")
         bias = keep.tile([P, TILES], F32, name="bias", tag="floor_bias")
@@ -246,9 +257,8 @@ def tile_picked_ylucb_soft_p_kernel(tc, x_words, x_scales, lc, th, alpha, offs, 
         def score(g):
             for t in (2 * g, 2 * g + 1):
                 n, i = divmod(t, TPH)
-                bon = bon_early[:, t, :] if g == 0 else bon_late[:, t - 2, :]
                 nc.vector.scalar_tensor_tensor(
-                    out=neg[:, t, :], in0=bon, scalar=alpha_sb[:, t : t + 1], in1=ys[n][:, i, :],
+                    out=neg[:, t, :], in0=bon[:, t, :], scalar=alpha_sb[:, t : t + 1], in1=ys[n][:, i, :],
                     op0=ALU.mult, op1=ALU.add,
                 )
 
@@ -256,30 +266,30 @@ def tile_picked_ylucb_soft_p_kernel(tc, x_words, x_scales, lc, th, alpha, offs, 
             t = slice(2 * g, 2 * g + 2)
             nc.vector.tensor_reduce(out=bias[:, t], in_=neg[:, t, :], axis=AX.X, op=ALU.min)
 
-        pairs = TILES // 2
-        score(0)
-        for g in range(1, pairs):
+        for g in order:
             score(g)
-            least(g - 1)
-        least(pairs - 1)
+        for g in range(4):
+            least(g)
 
         ex = keep.tile([P, TILES, V], F32, name="ex")
         inv = keep.tile([P, TILES], F32, name="inv", tag="zero_bon_late_inv")
         res = keep.tile([P, TILES, V], F32, name="res")
-        for t in range(TILES):
+        tiles = list(range(TILES))
+        for k, t in enumerate(tiles):
             total = keep.tile([P, 1], F32, name=f"total{t}")
             nc.scalar.activation(
                 out=ex[:, t, :], in_=neg[:, t, :], func=ACT.Exp, bias=bias[:, t : t + 1], scale=-1.0,
                 accum_out=total[:],
             )
             nc.vector.reciprocal(out=inv[:, t : t + 1], in_=total[:])
-            if t > 0:
+            if k > 0:
+                u = tiles[k - 1]
                 nc.vector.tensor_scalar(
-                    out=res[:, t - 1, :], in0=ex[:, t - 1, :], scalar1=inv[:, t - 1 : t], scalar2=None, op0=ALU.mult
+                    out=res[:, u, :], in0=ex[:, u, :], scalar1=inv[:, u : u + 1], scalar2=None, op0=ALU.mult
                 )
-        last = TILES - 1
+        last = tiles[-1]
         nc.scalar.activation(out=res[:, last, :], in_=ex[:, last, :], func=ACT.Copy, scale=inv[:, last : last + 1])
 
         out_v = out.rearrange("(i p) v -> p i v", p=P)
-        for lo, hi in ((0, 2), (2, 4), (4, 6), (6, 7), (7, 8)):
+        for lo, hi in ((0, 4), (4, 6), (6, 7), (7, 8)):
             nc.sync.dma_start(out=out_v[:, lo:hi, :], in_=res[:, lo:hi, :])

@@ -91,7 +91,7 @@ def tile_picked_ylucb_soft_p_kernel(tc, x_words, x_scales, lc, th, alpha, offs, 
 
         def cast_views(h, raw):
             bf = keep.tile([P, D, VH, PACK], BF16, name=f"lc_bf{h}", tag=f"lc_bf{h}", align_bytes=64)
-            return bf, bf[:].rearrange("p d v j -> p v j d"), raw[:].rearrange("p j (v d) -> p v j d", d=D)
+            return bf, bf[:].rearrange("p d v j -> p v d j"), raw[:].rearrange("p j (v d) -> p v d j", d=D)
 
         def quantise_half(h, bf):
             codes = keep.tile([P, WH], U32, name=f"lc_codes{h}", tag=f"lc_codes{h}", align_bytes=64)
@@ -134,9 +134,9 @@ def tile_picked_ylucb_soft_p_kernel(tc, x_words, x_scales, lc, th, alpha, offs, 
         x_picked = [gather_words(0), gather_words(1)]
         bf1, dst, src = cast_views(1, lc_raw1[0])
         nc.scalar.copy(out=dst[:, 0:S_CUT], in_=src)
-        nc.scalar.activation(
-            out=dst[:, S_CUT:VH], in_=lc_raw1[1][:].rearrange("p j (v d) -> p v j d", d=D), func=ACT.Copy, scale=unit[:]
-        )
+        src = lc_raw1[1][:].rearrange("p j (v d) -> p v d j", d=D)
+        nc.scalar.activation(out=dst[:, S_CUT : S_CUT + 8], in_=src[:, 0:8], func=ACT.Copy, scale=unit[:])
+        nc.scalar.copy(out=dst[:, S_CUT + 8 : VH], in_=src[:, 8 : VH - S_CUT])
         halves.append(quantise_half(1, bf1))
 
         def x_tile(t):
@@ -223,17 +223,17 @@ def tile_picked_ylucb_soft_p_kernel(tc, x_words, x_scales, lc, th, alpha, offs, 
         nc.vector.tensor_copy(out=z_sb[:], in_=z_last[:])
         add_first(0, 0, sq_a[0][:, 0:2, :])
         nc.vector.tensor_tensor(out=sq_last[:], in0=z_last[:], in1=z_sb[:], op=ALU.mult)
-        add_first(1, 0, sq_a[0][:, 2:4, :])
         add_first(0, 1, sq_a[1][:])
+        add_first(1, 0, sq_a[0][:, 2:4, :])
         transposed_squares(4, 0, (0, 1), 0.0)
         transposed_squares(5, 0, (2, 3), 0.0)
         transposed_squares(6, 1, (0, 1), 0.0)
-        ys = [products_with_th(0, 7), products_with_th(1, 0)]
+        ys = [products_with_th(0, 7)]
         z, sq = transposed_products(4, 1, (2, 3))
         nc.scalar.activation(out=sq[:, 0, :], in_=z[:, 0, :], func=ACT.Square, bias=zero_late[:])
         nc.scalar.activation(out=sq[:, 1, :], in_=z[:, 1, :], func=ACT.Square)
-        add_first(1, 1, sq_last[:])
         add_second(0)
+        add_first(1, 1, sq_last[:])
         add_second(1)
         sums_v = sums_a[:].rearrange("p t h v -> p t (h v)")
 
@@ -245,9 +245,10 @@ def tile_picked_ylucb_soft_p_kernel(tc, x_words, x_scales, lc, th, alpha, offs, 
                     is_transpose=True, start=(d == 0 and i == 0), stop=(d == D - 1 and i == 1),
                 )
 
+        ys.append(products_with_th(1, 4))
         bon = keep.tile([P, TILES, V], F32, name="bon", tag="zero_bon_late_inv")
         sums = (sums_v[:, 0:2, :], sums_v[:, 2:4, :], sums_b[0][:], sums_b[1][:])
-        order = (2, 0, 1, 3)
+        order = (0, 2, 3, 1)
         for g in order:
             nc.scalar.activation(out=bon[:, 2 * g : 2 * g + 2, :], in_=sums[g], func=ACT.Sqrt, bias=floor[:])
 
@@ -291,5 +292,5 @@ def tile_picked_ylucb_soft_p_kernel(tc, x_words, x_scales, lc, th, alpha, offs, 
         nc.scalar.activation(out=res[:, last, :], in_=ex[:, last, :], func=ACT.Copy, scale=inv[:, last : last + 1])
 
         out_v = out.rearrange("(i p) v -> p i v", p=P)
-        for lo, hi in ((0, 4), (4, 6), (6, 7), (7, 8)):
+        for lo, hi in ((0, 3), (3, 6), (6, 7), (7, 8)):
             nc.sync.dma_start(out=out_v[:, lo:hi, :], in_=res[:, lo:hi, :])

@@ -27,7 +27,7 @@ VH = V // 2
 WH = W // 2
 PAIR = 2 * P
 S_CUT = 32
-WARM_PASSES = 3
+WARM_PASSES = 2
 
 
 def tile_picked_ylucb_soft_p_kernel(tc, x_words, x_scales, lc, th, alpha, offs, out):
@@ -49,7 +49,6 @@ def tile_picked_ylucb_soft_p_kernel(tc, x_words, x_scales, lc, th, alpha, offs, 
 
         alpha_rows = keep.tile([P, P], F32, name="alpha_rows")
         nc.gpsimd.memset(alpha_rows[0 : P - TILES, :], 0.0)
-        nc.scalar.dma_start(out=alpha_rows[P - TILES : P, :], in_=alpha.rearrange("(i p) o -> i (p o)", p=P))
 
         one = keep.tile([P, 2], F32, name="one")
         nc.gpsimd.memset(one[:, 0:1], 1.0)
@@ -67,6 +66,8 @@ def tile_picked_ylucb_soft_p_kernel(tc, x_words, x_scales, lc, th, alpha, offs, 
         nc.sync.dma_start(out=lc_raw0[:], in_=lc_rows[:, :, 0:WH])
         x_table = keep.tile([P, T], U32, name="x_table", tag="words_pair", align_bytes=64)
         nc.sync.dma_start(out=x_table[:].bitcast(I32), in_=x_words[0].rearrange("p n t -> p (n t)").bitcast(I32))
+
+        nc.sync.dma_start(out=alpha_rows[P - TILES : P, :], in_=alpha.rearrange("(i p) o -> i (p o)", p=P))
 
         x_plane = keep.tile([P, S], U8, name="x_plane", align_bytes=64)
         nc.vector.memset(x_plane[:].bitcast(I32), 0)
@@ -89,17 +90,22 @@ def tile_picked_ylucb_soft_p_kernel(tc, x_words, x_scales, lc, th, alpha, offs, 
         by_d_codes = keep.tile([P, D, 2, VH], U32, name="by_d_codes", align_bytes=64)
         by_d_plane = keep.tile([P, D, 2, VH], U8, name="by_d_plane", align_bytes=64)
 
-        def cast_views(h, raw):
+        def cast_views(h):
             bf = keep.tile([P, D, VH, PACK], BF16, name=f"lc_bf{h}", tag=f"lc_bf{h}", align_bytes=64)
-            return bf, bf[:].rearrange("p d v j -> p v d j"), raw[:].rearrange("p j (v d) -> p v d j", d=D)
+            return bf, bf[:].rearrange("p d v (e j) -> p v e d j", e=2)
 
-        def quantise_half(h, bf):
+        def raw_view(raw):
+            return raw[:].rearrange("p (e j) (v d) -> p v e d j", e=2, d=D)
+
+        def quantise_half(h, bf, between=None):
             codes = keep.tile([P, WH], U32, name=f"lc_codes{h}", tag=f"lc_codes{h}", align_bytes=64)
             plane = keep.tile([P, WH], U8, name=f"lc_plane{h}", align_bytes=64)
             nc.vector.memset(plane[:].bitcast(I32), 0)
             nc.vector.quantize_mx(
                 out=codes[:].bitcast(FP8X4), scales=plane[:], in_=bf[:].rearrange("p d v j -> p (d v j)")
             )
+            if between:
+                between()
             nc.vector.tensor_copy(out=by_d_codes[:, :, h, :], in_=codes[:].rearrange("p (d v) -> p d v", d=D))
             nc.vector.tensor_copy(
                 out=by_d_plane[:, :, h, :].bitcast(I32), in_=plane[:].rearrange("p (d v) -> p d v", d=D).bitcast(I32)
@@ -107,40 +113,45 @@ def tile_picked_ylucb_soft_p_kernel(tc, x_words, x_scales, lc, th, alpha, offs, 
             return codes, plane
 
         def gather_words(n):
-            picked = keep.tile([P, HALF], U32, name=f"x_picked{n}", align_bytes=64)
-            cols = HALF // 16
+            picked = keep.tile([P, PAIR], U32, name=f"x_picked{n}", align_bytes=64)
+            cols = PAIR // 16
             nc.vector.tensor_copy(picked[:], x_table[:].indirect(offsets[:, n * cols : (n + 1) * cols]))
             return picked
 
-        bf0, dst, src = cast_views(0, lc_raw0)
-        nc.scalar.copy(out=dst, in_=src)
+        bf0, dst = cast_views(0)
+        nc.scalar.copy(out=dst, in_=raw_view(lc_raw0))
         th_raw = keep.tile([P, PACK, V], F32, name="th_raw", tag="lc0_th")
         nc.sync.dma_start(out=th_raw[:], in_=th.rearrange("(p j) w -> p j w", j=PACK))
         halves = [quantise_half(0, bf0)]
 
-        alpha_t = bank(7, [P, P])
-        nc.tensor.transpose(alpha_t[:], alpha_rows[:], ident[:])
-        alpha_sb = keep.tile([P, TILES], F32, name="alpha_sb")
-        nc.scalar.activation(out=alpha_sb[:], in_=alpha_t[:, P - TILES : P], func=ACT.Copy, scale=-2.0)
-
-        scratch = bank(6, [P, WH])
+        alpha_t = bank(6, [P, 2, WH])
+        nc.tensor.transpose(alpha_t[:, 0, 0:P], alpha_rows[:], ident[:])
         codes, plane = halves[0]
         for w in range(WARM_PASSES):
             nc.tensor.matmul_mx(
-                out=scratch[:], lhsT=codes[:, 0:P].bitcast(FP8X4), lhsT_scale=plane[:, 0:P],
-                rhs=codes[:].bitcast(FP8X4), rhs_scale=x_plane[:, 0:WH], start=True, stop=True,
+                out=alpha_t[:, 1, :], lhsT=codes[:, 0:P].bitcast(FP8X4), lhsT_scale=plane[:, 0:P],
+                rhs=codes[:].bitcast(FP8X4), rhs_scale=plane[:], start=True, stop=True,
             )
 
-        x_picked = [gather_words(0), gather_words(1)]
-        bf1, dst, src = cast_views(1, lc_raw1[0])
-        nc.scalar.copy(out=dst[:, 0:S_CUT], in_=src)
-        src = lc_raw1[1][:].rearrange("p j (v d) -> p v d j", d=D)
-        nc.scalar.activation(out=dst[:, S_CUT : S_CUT + 8], in_=src[:, 0:8], func=ACT.Copy, scale=unit[:])
-        nc.scalar.copy(out=dst[:, S_CUT + 8 : VH], in_=src[:, 8 : VH - S_CUT])
-        halves.append(quantise_half(1, bf1))
+        x_picked = [gather_words(n) for n in range(4)]
+        bf1, dst = cast_views(1)
+        nc.scalar.copy(out=dst[:, 0:S_CUT], in_=raw_view(lc_raw1[0]))
+        nc.scalar.activation(
+            out=bf1[:].rearrange("p d v j -> p v d j")[:, S_CUT : S_CUT + 8],
+            in_=lc_raw1[1][:].rearrange("p j (v d) -> p v d j", d=D)[:, 0:8], func=ACT.Copy, scale=unit[:],
+        )
+        nc.scalar.copy(out=dst[:, S_CUT + 8 : VH], in_=raw_view(lc_raw1[1])[:, 8 : VH - S_CUT])
+        alpha_sb = placed.tile([P, TILES], F32, name="alpha_sb", offset=2048, align_bytes=64)
+
+        def copy_alpha():
+            nc.vector.tensor_scalar(
+                out=alpha_sb[:], in0=alpha_t[:, 0, P - TILES : P], scalar1=-2.0, scalar2=None, op0=ALU.mult
+            )
+
+        halves.append(quantise_half(1, bf1, copy_alpha))
 
         def x_tile(t):
-            n, i = divmod(t, TPH)
+            n, i = divmod(t, 2)
             return x_picked[n][:, i * P : (i + 1) * P].bitcast(FP8X4), x_plane[:, t * P : (t + 1) * P]
 
         sq_a = [
@@ -165,7 +176,8 @@ def tile_picked_ylucb_soft_p_kernel(tc, x_words, x_scales, lc, th, alpha, offs, 
 
         th_bf = keep.tile([P, V, PACK], BF16, name="th_bf", tag="lc_bf1", align_bytes=64)
         nc.vector.tensor_scalar(
-            out=th_bf[:], in0=th_raw[:].rearrange("p j v -> p v j"), scalar1=-2.0, scalar2=None, op0=ALU.mult
+            out=th_bf[:].rearrange("p (c i) j -> p c j i", i=4), in0=th_raw[:].rearrange("p j (c i) -> p c j i", i=4),
+            scalar1=-2.0, scalar2=None, op0=ALU.mult,
         )
         pair = keep.tile([P, 2, TPH, 2 * VH], F32, name="pair", tag="words_pair", align_bytes=64)
         sums_a = keep.tile([P, TPH, 2, VH], F32, name="sums_a")
@@ -196,7 +208,7 @@ def tile_picked_ylucb_soft_p_kernel(tc, x_words, x_scales, lc, th, alpha, offs, 
                 nc.tensor.matmul_mx(
                     out=z[:, j, :], lhsT=by_d_codes[:, d].rearrange("p h v -> p (h v)").bitcast(FP8X4),
                     lhsT_scale=by_d_plane[:, d].rearrange("p h v -> p (h v)"),
-                    rhs=x_picked[1][:, g * PAIR : (g + 1) * PAIR].bitcast(FP8X4),
+                    rhs=x_picked[2 + g][:].bitcast(FP8X4),
                     rhs_scale=x_plane[:, HALF + g * PAIR : HALF + (g + 1) * PAIR], start=True, stop=True,
                 )
             sq = keep.tile([P, len(ds), PAIR], F32, name=f"sq_b{g}{ds[0]}")

@@ -73,16 +73,17 @@ def tile_picked_ylucb_soft_p_kernel(tc, x_words, x_scales, lc, th, alpha, offs, 
         nc.vector.memset(x_plane[:].bitcast(I32), 0)
         sc_picked = keep.tile([P, S], U8, name="sc_picked", align_bytes=64)
         nc.vector.tensor_copy(sc_picked[:], sc_table[:].indirect(offsets[:]))
-        for q in range(4):
-            first = P - SCALE_ROWS + 4 * q
-            nc.sync.dma_start(
-                out=x_plane[32 * q : 32 * q + 4, :].bitcast(I32), in_=sc_picked[first : first + 4, :].bitcast(I32)
-            )
         lc_raw1 = []
         for n in range(2):
             raw = placed.tile([P, PACK, WH // 2], F32, name=f"lc_raw1{n}", offset=2048 * n, align_bytes=64)
             nc.sync.dma_start(out=raw[:], in_=lc_rows[:, :, WH + n * WH // 2 : WH + (n + 1) * WH // 2])
             lc_raw1.append(raw)
+
+        for q in range(4):
+            first = P - SCALE_ROWS + 4 * q
+            nc.sync.dma_start(
+                out=x_plane[32 * q : 32 * q + 4, :].bitcast(I32), in_=sc_picked[first : first + 4, :].bitcast(I32)
+            )
 
         ident = keep.tile([P, P], F32, name="ident")
         make_identity(nc, ident[:])

@@ -98,15 +98,13 @@ def tile_picked_ylucb_soft_p_kernel(tc, x_words, x_scales, lc, th, alpha, offs, 
         def raw_view(raw):
             return raw[:].rearrange("p (e j) (v d) -> p v e d j", e=2, d=D)
 
-        def quantise_half(h, bf, between=None):
+        def quantise_half(h, bf):
             codes = keep.tile([P, WH], U32, name=f"lc_codes{h}", tag=f"lc_codes{h}", align_bytes=64)
             plane = keep.tile([P, WH], U8, name=f"lc_plane{h}", align_bytes=64)
             nc.vector.memset(plane[:].bitcast(I32), 0)
             nc.vector.quantize_mx(
                 out=codes[:].bitcast(FP8X4), scales=plane[:], in_=bf[:].rearrange("p d v j -> p (d v j)")
             )
-            if between:
-                between()
             nc.vector.tensor_copy(out=by_d_codes[:, :, h, :], in_=codes[:].rearrange("p (d v) -> p d v", d=D))
             nc.vector.tensor_copy(
                 out=by_d_plane[:, :, h, :].bitcast(I32), in_=plane[:].rearrange("p (d v) -> p d v", d=D).bitcast(I32)
@@ -127,6 +125,8 @@ def tile_picked_ylucb_soft_p_kernel(tc, x_words, x_scales, lc, th, alpha, offs, 
 
         alpha_t = bank(6, [P, 2, WH])
         nc.tensor.transpose(alpha_t[:, 0, 0:P], alpha_rows[:], ident[:])
+        alpha_sb = keep.tile([P, TILES], F32, name="alpha_sb")
+        nc.scalar.activation(out=alpha_sb[:], in_=alpha_t[:, 0, P - TILES : P], func=ACT.Copy, scale=-2.0)
         codes, plane = halves[0]
         for w in range(WARM_PASSES):
             nc.tensor.matmul_mx(
@@ -142,14 +142,7 @@ def tile_picked_ylucb_soft_p_kernel(tc, x_words, x_scales, lc, th, alpha, offs, 
             in_=lc_raw1[1][:].rearrange("p j (v d) -> p v d j", d=D)[:, 0:8], func=ACT.Copy, scale=unit[:],
         )
         nc.scalar.copy(out=dst[:, S_CUT + 8 : VH], in_=raw_view(lc_raw1[1])[:, 8 : VH - S_CUT])
-        alpha_sb = placed.tile([P, TILES], F32, name="alpha_sb", offset=2048, align_bytes=64)
-
-        def copy_alpha():
-            nc.vector.tensor_scalar(
-                out=alpha_sb[:], in0=alpha_t[:, 0, P - TILES : P], scalar1=-2.0, scalar2=None, op0=ALU.mult
-            )
-
-        halves.append(quantise_half(1, bf1, copy_alpha))
+        halves.append(quantise_half(1, bf1))
 
         def x_tile(t):
             n, i = divmod(t, 2)

@@ -20,13 +20,14 @@ AX = mybir.AxisListType
 P = 128
 PACK = 4
 SCALE_ROWS = K // 32
-HALF = S // 2
 TILES = S // P
-TPH = TILES // 2
+DIRECT = TILES // 2
 VH = V // 2
+VQ = V // 4
 WH = W // 2
+WQ = W // 4
 PAIR = 2 * P
-S_CUT = 32
+HOLD_ARMS = 8
 WARM_PASSES = 2
 
 
@@ -75,11 +76,11 @@ def tile_picked_ylucb_soft_p_kernel(tc, x_words, x_scales, lc, th, alpha, offs, 
         nc.vector.tensor_copy(sc_picked[:], sc_table[:].indirect(offsets[:]))
         lc_raw1 = []
         for n in range(2):
-            raw = placed.tile([P, PACK, WH // 2], F32, name=f"lc_raw1{n}", offset=2048 * n, align_bytes=64)
-            nc.sync.dma_start(out=raw[:], in_=lc_rows[:, :, WH + n * WH // 2 : WH + (n + 1) * WH // 2])
+            raw = placed.tile([P, PACK, WQ], F32, name=f"lc_raw1{n}", offset=n * T // 2, align_bytes=64)
+            nc.sync.dma_start(out=raw[:], in_=lc_rows[:, :, WH + n * WQ : WH + (n + 1) * WQ])
             lc_raw1.append(raw)
 
-        for q in range(4):
+        for q in range(SCALE_ROWS // 4):
             first = P - SCALE_ROWS + 4 * q
             nc.sync.dma_start(
                 out=x_plane[32 * q : 32 * q + 4, :].bitcast(I32), in_=sc_picked[first : first + 4, :].bitcast(I32)
@@ -92,29 +93,33 @@ def tile_picked_ylucb_soft_p_kernel(tc, x_words, x_scales, lc, th, alpha, offs, 
         by_d_plane = keep.tile([P, D, 2, VH], U8, name="by_d_plane", align_bytes=64)
 
         def cast_views(h):
-            bf = keep.tile([P, D, VH, PACK], BF16, name=f"lc_bf{h}", tag=f"lc_bf{h}", align_bytes=64)
+            bf = keep.tile([P, D, VH, PACK], BF16, name=f"lc_bf{h}", align_bytes=64)
             return bf, bf[:].rearrange("p d v (e j) -> p v e d j", e=2)
 
         def raw_view(raw):
             return raw[:].rearrange("p (e j) (v d) -> p v e d j", e=2, d=D)
 
-        def quantise_half(h, bf):
-            codes = keep.tile([P, WH], U32, name=f"lc_codes{h}", tag=f"lc_codes{h}", align_bytes=64)
+        def half_tiles(h):
+            codes = keep.tile([P, WH], U32, name=f"lc_codes{h}", align_bytes=64)
             plane = keep.tile([P, WH], U8, name=f"lc_plane{h}", align_bytes=64)
-            nc.vector.memset(plane[:].bitcast(I32), 0)
+            return codes, plane
+
+        def quantise_half(h, bf):
+            codes, plane = half_tiles(h)
             nc.vector.quantize_mx(
                 out=codes[:].bitcast(FP8X4), scales=plane[:], in_=bf[:].rearrange("p d v j -> p (d v j)")
             )
-            nc.vector.tensor_copy(out=by_d_codes[:, :, h, :], in_=codes[:].rearrange("p (d v) -> p d v", d=D))
-            nc.vector.tensor_copy(
-                out=by_d_plane[:, :, h, :].bitcast(I32), in_=plane[:].rearrange("p (d v) -> p d v", d=D).bitcast(I32)
-            )
+            for d in range(D):
+                nc.vector.quantize_mx(
+                    out=by_d_codes[:, d, h, :].bitcast(FP8X4), scales=by_d_plane[:, d, h, :],
+                    in_=bf[:, d].rearrange("p v j -> p (v j)"),
+                )
             return codes, plane
 
-        def gather_words(n):
-            picked = keep.tile([P, PAIR], U32, name=f"x_picked{n}", align_bytes=64)
+        def gather_words(g):
+            picked = keep.tile([P, PAIR], U32, name=f"x_picked{g}", align_bytes=64)
             cols = PAIR // 16
-            nc.vector.tensor_copy(picked[:], x_table[:].indirect(offsets[:, n * cols : (n + 1) * cols]))
+            nc.vector.tensor_copy(picked[:], x_table[:].indirect(offsets[:, g * cols : (g + 1) * cols]))
             return picked
 
         bf0, dst = cast_views(0)
@@ -134,26 +139,26 @@ def tile_picked_ylucb_soft_p_kernel(tc, x_words, x_scales, lc, th, alpha, offs, 
                 rhs=codes[:].bitcast(FP8X4), rhs_scale=plane[:], start=True, stop=True,
             )
 
-        x_picked = [gather_words(n) for n in range(4)]
+        x_picked = [gather_words(g) for g in range(TILES // 2)]
         bf1, dst = cast_views(1)
-        nc.scalar.copy(out=dst[:, 0:S_CUT], in_=raw_view(lc_raw1[0]))
+        nc.scalar.copy(out=dst[:, 0:VQ], in_=raw_view(lc_raw1[0]))
         nc.scalar.activation(
-            out=bf1[:].rearrange("p d v j -> p v d j")[:, S_CUT : S_CUT + 8],
-            in_=lc_raw1[1][:].rearrange("p j (v d) -> p v d j", d=D)[:, 0:8], func=ACT.Copy, scale=unit[:],
+            out=bf1[:].rearrange("p d v j -> p v d j")[:, VQ : VQ + HOLD_ARMS],
+            in_=lc_raw1[1][:].rearrange("p j (v d) -> p v d j", d=D)[:, 0:HOLD_ARMS], func=ACT.Copy, scale=unit[:],
         )
-        nc.scalar.copy(out=dst[:, S_CUT + 8 : VH], in_=raw_view(lc_raw1[1])[:, 8 : VH - S_CUT])
+        nc.scalar.copy(out=dst[:, VQ + HOLD_ARMS : VH], in_=raw_view(lc_raw1[1])[:, HOLD_ARMS:VQ])
         halves.append(quantise_half(1, bf1))
 
         def x_tile(t):
-            n, i = divmod(t, 2)
-            return x_picked[n][:, i * P : (i + 1) * P].bitcast(FP8X4), x_plane[:, t * P : (t + 1) * P]
+            g, i = divmod(t, 2)
+            return x_picked[g][:, i * P : (i + 1) * P].bitcast(FP8X4), x_plane[:, t * P : (t + 1) * P]
 
         sq_a = [
-            keep.tile([P, TPH, WH], F32, name="sq_a0", tag="unit_sq0"),
+            keep.tile([P, DIRECT, WH], F32, name="sq_a0", tag="unit_sq0"),
             keep.tile([P, 2, WH], F32, name="sq_a1"),
         ]
 
-        def direct_squares(h, b, lo, hi):
+        def direct_products(h, b, lo, hi):
             codes, plane = halves[h]
             z = bank(b, [P, hi - lo, WH])
             for t in range(lo, hi):
@@ -165,28 +170,27 @@ def tile_picked_ylucb_soft_p_kernel(tc, x_words, x_scales, lc, th, alpha, offs, 
             return z
 
         for h, b, lo, hi in ((0, 7, 0, 1), (0, 0, 1, 2), (0, 1, 2, 4), (1, 2, 0, 2)):
-            nc.scalar.activation(out=sq_a[h][:, lo:hi, :], in_=direct_squares(h, b, lo, hi)[:], func=ACT.Square)
-        z_last = direct_squares(1, 3, 2, 4)
+            nc.scalar.activation(out=sq_a[h][:, lo:hi, :], in_=direct_products(h, b, lo, hi)[:], func=ACT.Square)
 
-        th_bf = keep.tile([P, V, PACK], BF16, name="th_bf", tag="lc_bf1", align_bytes=64)
+        th_bf = placed.tile([P, V, PACK], BF16, name="th_bf", offset=T // 2, align_bytes=64)
         nc.vector.tensor_scalar(
             out=th_bf[:].rearrange("p (c i) j -> p c j i", i=4), in0=th_raw[:].rearrange("p j (c i) -> p c j i", i=4),
             scalar1=-2.0, scalar2=None, op0=ALU.mult,
         )
-        pair = keep.tile([P, 2, TPH, 2 * VH], F32, name="pair", tag="words_pair", align_bytes=64)
-        sums_a = keep.tile([P, TPH, 2, VH], F32, name="sums_a")
+        partial = keep.tile([P, 2, DIRECT, 2 * VH], F32, name="pair", tag="words_pair", align_bytes=64)
+        sums_a = keep.tile([P, DIRECT, 2, VH], F32, name="sums_a")
 
         def add_first(g, h, sq):
             t = slice(2 * g, 2 * g + 2)
             nc.vector.tensor_tensor(
-                out=pair[:, h, t, :], in0=sq[:, :, 0 : 2 * VH], in1=sq[:, :, 2 * VH : 4 * VH], op=ALU.add
+                out=partial[:, h, t, :], in0=sq[:, :, 0 : 2 * VH], in1=sq[:, :, 2 * VH : 4 * VH], op=ALU.add
             )
 
         def add_second(g):
             t = slice(2 * g, 2 * g + 2)
             nc.vector.tensor_tensor(
-                out=sums_a[:, t].rearrange("p t h v -> p h t v"), in0=pair[:, :, t, 0:VH],
-                in1=pair[:, :, t, VH : 2 * VH], op=ALU.add,
+                out=sums_a[:, t].rearrange("p t h v -> p h t v"), in0=partial[:, :, t, 0:VH],
+                in1=partial[:, :, t, VH : 2 * VH], op=ALU.add,
             )
 
         th_codes = keep.tile([P, V], U32, name="th_codes", align_bytes=64)
@@ -202,28 +206,30 @@ def tile_picked_ylucb_soft_p_kernel(tc, x_words, x_scales, lc, th, alpha, offs, 
                 nc.tensor.matmul_mx(
                     out=z[:, j, :], lhsT=by_d_codes[:, d].rearrange("p h v -> p (h v)").bitcast(FP8X4),
                     lhsT_scale=by_d_plane[:, d].rearrange("p h v -> p (h v)"),
-                    rhs=x_picked[2 + g][:].bitcast(FP8X4),
-                    rhs_scale=x_plane[:, HALF + g * PAIR : HALF + (g + 1) * PAIR], start=True, stop=True,
+                    rhs=x_picked[g][:].bitcast(FP8X4),
+                    rhs_scale=x_plane[:, g * PAIR : (g + 1) * PAIR], start=True, stop=True,
                 )
-            sq = keep.tile([P, len(ds), PAIR], F32, name=f"sq_b{g}{ds[0]}")
+            sq = keep.tile([P, len(ds), PAIR], F32, name=f"sq_b{g - 2}{ds[0]}")
             for j, d in enumerate(ds):
                 sq_b[g, d] = sq[:, j, :]
             return z, sq
 
-        def transposed_squares(b, g, ds, nought):
+        def transposed_squares(b, g, ds):
             z, sq = transposed_products(b, g, ds)
-            nc.scalar.activation(out=sq[:], in_=z[:], func=ACT.Square, bias=nought)
+            nc.scalar.activation(out=sq[:], in_=z[:], func=ACT.Square, bias=0.0)
 
         def products_with_th(n, b):
-            y = bank(b, [P, TPH, V])
-            for i in range(TPH):
-                x_codes, x_scale = x_tile(n * TPH + i)
+            y = bank(b, [P, DIRECT, V])
+            for i in range(DIRECT):
+                x_codes, x_scale = x_tile(n * DIRECT + i)
                 nc.tensor.matmul_mx(
                     out=y[:, i, :], lhsT=x_codes, lhsT_scale=x_scale, rhs=th_codes[:].bitcast(FP8X4),
                     rhs_scale=th_plane[:], start=True, stop=True,
                 )
             return y
 
+        transposed_squares(4, 2, (0, 1))
+        z_last = direct_products(1, 3, 2, 4)
         z_sb = keep.tile([P, 2, WH], F32, name="z_sb")
         sq_last = keep.tile([P, 2, WH], F32, name="sq_last")
         nc.vector.tensor_copy(out=z_sb[:], in_=z_last[:])
@@ -231,11 +237,10 @@ def tile_picked_ylucb_soft_p_kernel(tc, x_words, x_scales, lc, th, alpha, offs, 
         nc.vector.tensor_tensor(out=sq_last[:], in0=z_last[:], in1=z_sb[:], op=ALU.mult)
         add_first(0, 1, sq_a[1][:])
         add_first(1, 0, sq_a[0][:, 2:4, :])
-        transposed_squares(4, 0, (0, 1), 0.0)
-        transposed_squares(5, 0, (2, 3), 0.0)
-        transposed_squares(6, 1, (0, 1), 0.0)
+        transposed_squares(5, 2, (2, 3))
+        transposed_squares(6, 3, (0, 1))
         ys = [products_with_th(0, 7)]
-        z, sq = transposed_products(4, 1, (2, 3))
+        z, sq = transposed_products(4, 3, (2, 3))
         nc.scalar.activation(out=sq[:, 0, :], in_=z[:, 0, :], func=ACT.Square, bias=zero_late[:])
         nc.scalar.activation(out=sq[:, 1, :], in_=z[:, 1, :], func=ACT.Square)
         add_second(0)
@@ -243,17 +248,18 @@ def tile_picked_ylucb_soft_p_kernel(tc, x_words, x_scales, lc, th, alpha, offs, 
         add_second(1)
         sums_v = sums_a[:].rearrange("p t h v -> p t (h v)")
 
-        sums_b = [bank(1 + g, [P, 2, V]) for g in range(2)]
-        for g, d in [(g, d) for g in range(2) for d in range(D)]:
-            for i in range(2):
-                nc.tensor.matmul(
-                    out=sums_b[g][:, i, :], lhsT=sq_b[g, d][:, i * P : (i + 1) * P], rhs=ident[:],
-                    is_transpose=True, start=(d == 0 and i == 0), stop=(d == D - 1 and i == 1),
-                )
+        sums_b = {g: bank(g - 1, [P, 2, V]) for g in (2, 3)}
+        for g in (2, 3):
+            for d in range(D):
+                for i in range(2):
+                    nc.tensor.matmul(
+                        out=sums_b[g][:, i, :], lhsT=sq_b[g, d][:, i * P : (i + 1) * P], rhs=ident[:],
+                        is_transpose=True, start=(d == 0 and i == 0), stop=(d == D - 1 and i == 1),
+                    )
 
         ys.append(products_with_th(1, 4))
         bon = keep.tile([P, TILES, V], F32, name="bon", tag="zero_bon_late_inv")
-        sums = (sums_v[:, 0:2, :], sums_v[:, 2:4, :], sums_b[0][:], sums_b[1][:])
+        sums = (sums_v[:, 0:2, :], sums_v[:, 2:4, :], sums_b[2][:], sums_b[3][:])
         order = (0, 2, 3, 1)
         for g in order:
             nc.scalar.activation(out=bon[:, 2 * g : 2 * g + 2, :], in_=sums[g], func=ACT.Sqrt, bias=floor[:])
@@ -263,7 +269,7 @@ def tile_picked_ylucb_soft_p_kernel(tc, x_words, x_scales, lc, th, alpha, offs, 
 
         def score(g):
             for t in (2 * g, 2 * g + 1):
-                n, i = divmod(t, TPH)
+                n, i = divmod(t, DIRECT)
                 nc.vector.scalar_tensor_tensor(
                     out=neg[:, t, :], in0=bon[:, t, :], scalar=alpha_sb[:, t : t + 1], in1=ys[n][:, i, :],
                     op0=ALU.mult, op1=ALU.add,
@@ -275,26 +281,25 @@ def tile_picked_ylucb_soft_p_kernel(tc, x_words, x_scales, lc, th, alpha, offs, 
 
         for g in order:
             score(g)
-        for g in range(4):
+        for g in range(TILES // 2):
             least(g)
 
         ex = keep.tile([P, TILES, V], F32, name="ex")
         inv = keep.tile([P, TILES], F32, name="inv", tag="zero_bon_late_inv")
         res = keep.tile([P, TILES, V], F32, name="res")
-        tiles = list(range(TILES))
-        for k, t in enumerate(tiles):
+        for t in range(TILES):
             total = keep.tile([P, 1], F32, name=f"total{t}")
             nc.scalar.activation(
                 out=ex[:, t, :], in_=neg[:, t, :], func=ACT.Exp, bias=bias[:, t : t + 1], scale=-1.0,
                 accum_out=total[:],
             )
             nc.vector.reciprocal(out=inv[:, t : t + 1], in_=total[:])
-            if k > 0:
-                u = tiles[k - 1]
+            if t > 0:
+                u = t - 1
                 nc.vector.tensor_scalar(
                     out=res[:, u, :], in0=ex[:, u, :], scalar1=inv[:, u : u + 1], scalar2=None, op0=ALU.mult
                 )
-        last = tiles[-1]
+        last = TILES - 1
         nc.scalar.activation(out=res[:, last, :], in_=ex[:, last, :], func=ACT.Copy, scale=inv[:, last : last + 1])
 
         out_v = out.rearrange("(i p) v -> p i v", p=P)

@@ -132,12 +132,6 @@ def tile_picked_ylucb_soft_p_kernel(tc, x_words, x_scales, lc, th, alpha, offs, 
         nc.tensor.transpose(alpha_t[:, 0, 0:P], alpha_rows[:], ident[:])
         alpha_sb = keep.tile([P, TILES], F32, name="alpha_sb")
         nc.scalar.activation(out=alpha_sb[:], in_=alpha_t[:, 0, P - TILES : P], func=ACT.Copy, scale=-2.0)
-        codes, plane = halves[0]
-        for w in range(WARM_PASSES):
-            nc.tensor.matmul_mx(
-                out=alpha_t[:, 1, :], lhsT=codes[:, 0:P].bitcast(FP8X4), lhsT_scale=plane[:, 0:P],
-                rhs=codes[:].bitcast(FP8X4), rhs_scale=plane[:], start=True, stop=True,
-            )
 
         x_picked = [gather_words(g) for g in range(TILES // 2)]
         bf1, dst = cast_views(1)

from contextlib import ExitStack

import concourse.mybir as mybir
from concourse.masks import make_identity

K, T, S, V, D, W = 512, 4096, 1024, 128, 4, 512
FLOPS = 2 * K * S * (V + W)

F32 = mybir.dt.float32
BF16 = mybir.dt.bfloat16
I32 = mybir.dt.int32
U32 = mybir.dt.uint32
U16 = mybir.dt.uint16
U8 = mybir.dt.uint8
FP8X4 = mybir.dt.float8_e4m3fn_x4
ACT = mybir.ActivationFunctionType
ALU = mybir.AluOpType
AX = mybir.AxisListType

P = 128
PACK = 4
SCALE_ROWS = K // 32
TILES = S // P
DIRECT = TILES // 2
VH = V // 2
VQ = V // 4
WH = W // 2
WQ = W // 4
PAIR = 2 * P
HOLD_ARMS = 8
WARM_PASSES = 2


def tile_picked_ylucb_soft_p_kernel(tc, x_words, x_scales, lc, th, alpha, offs, out):
    nc = tc.nc
    with ExitStack() as ctx:
        keep = ctx.enter_context(tc.tile_pool(name="keep", bufs=1))
        placed = ctx.enter_context(tc.tile_pool(name="placed", bufs=1))
        psum = ctx.enter_context(tc.psum_pool(name="psum", bufs=1))

        def bank(b, shape):
            return psum.tile(shape, F32, name=f"bank{b}", tag=f"bank{b}")

        offsets = keep.tile([P, S // 16], U16, name="offsets")
        nc.sync.dma_start(offsets[:], offs)

        sc_table = placed.tile([P, T], U8, name="sc_table", offset=0, align_bytes=64)
        nc.sync.dma_start(out=sc_table[P - SCALE_ROWS : P, :].bitcast(I32), in_=x_scales[0].bitcast(I32))
        nc.vector.memset(sc_table[0 : P - SCALE_ROWS, :].bitcast(I32), 0)

        alpha_rows = keep.tile([P, P], F32, name="alpha_rows")
        nc.gpsimd.memset(alpha_rows[0 : P - TILES, :], 0.0)

        one = keep.tile([P, 2], F32, name="one")
        nc.gpsimd.memset(one[:, 0:1], 1.0)
        nc.scalar.activation(out=one[:, 1:2], in_=one[:, 0:1], func=ACT.Sqrt)

        floor = keep.tile([P, 1], F32, name="floor", tag="floor_bias")
        nc.gpsimd.tensor_scalar(out=floor[:], in0=one[:, 0:1], scalar1=0.05, scalar2=0.0, op0=ALU.mult, op1=ALU.add)
        unit = keep.tile([P, 1], F32, name="unit", tag="unit_sq0")
        nc.gpsimd.memset(unit[:], 1.0)
        zero_late = keep.tile([P, 1], F32, name="zero_late", tag="zero_bon_late_inv")
        nc.gpsimd.memset(zero_late[:], 0.0)

        lc_rows = lc.rearrange("(p j) w -> p j w", j=PACK)
        lc_raw0 = keep.tile([P, PACK, WH], F32, name="lc_raw0", tag="lc0_th")
        nc.sync.dma_start(out=lc_raw0[:], in_=lc_rows[:, :, 0:WH])
        x_table = keep.tile([P, T], U32, name="x_table", tag="words_pair", align_bytes=64)
        nc.sync.dma_start(out=x_table[:].bitcast(I32), in_=x_words[0].rearrange("p n t -> p (n t)").bitcast(I32))

        nc.sync.dma_start(out=alpha_rows[P - TILES : P, :], in_=alpha.rearrange("(i p) o -> i (p o)", p=P))

        x_plane = keep.tile([P, S], U8, name="x_plane", align_bytes=64)
        nc.vector.memset(x_plane[:].bitcast(I32), 0)
        sc_picked = keep.tile([P, S], U8, name="sc_picked", align_bytes=64)
        nc.vector.tensor_copy(sc_picked[:], sc_table[:].indirect(offsets[:]))
        lc_raw1 = []
        for n in range(2):
            raw = placed.tile([P, PACK, WQ], F32, name=f"lc_raw1{n}", offset=n * T // 2, align_bytes=64)
            nc.sync.dma_start(out=raw[:], in_=lc_rows[:, :, WH + n * WQ : WH + (n + 1) * WQ])
            lc_raw1.append(raw)

        for q in range(SCALE_ROWS // 4):
            first = P - SCALE_ROWS + 4 * q
            nc.sync.dma_start(
                out=x_plane[32 * q : 32 * q + 4, :].bitcast(I32), in_=sc_picked[first : first + 4, :].bitcast(I32)
            )

        ident = keep.tile([P, P], F32, name="ident")
        make_identity(nc, ident[:])

        by_d_codes = keep.tile([P, D, 2, VH], U32, name="by_d_codes", align_bytes=64)
        by_d_plane = keep.tile([P, D, 2, VH], U8, name="by_d_plane", align_bytes=64)

        def cast_views(h):
            bf = keep.tile([P, D, VH, PACK], BF16, name=f"lc_bf{h}", align_bytes=64)
            return bf, bf[:].rearrange("p d v (e j) -> p v e d j", e=2)

        def raw_view(raw):
            return raw[:].rearrange("p (e j) (v d) -> p v e d j", e=2, d=D)

        def half_tiles(h):
            codes = keep.tile([P, WH], U32, name=f"lc_codes{h}", align_bytes=64)
            plane = keep.tile([P, WH], U8, name=f"lc_plane{h}", align_bytes=64)
            return codes, plane

        def quantise_half(h, bf):
            codes, plane = half_tiles(h)
            nc.vector.quantize_mx(
                out=codes[:].bitcast(FP8X4), scales=plane[:], in_=bf[:].rearrange("p d v j -> p (d v j)")
            )
            for d in range(D):
                nc.vector.quantize_mx(
                    out=by_d_codes[:, d, h, :].bitcast(FP8X4), scales=by_d_plane[:, d, h, :],
                    in_=bf[:, d].rearrange("p v j -> p (v j)"),
                )
            return codes, plane

        def gather_words(g):
            picked = keep.tile([P, PAIR], U32, name=f"x_picked{g}", align_bytes=64)
            cols = PAIR // 16
            nc.vector.tensor_copy(picked[:], x_table[:].indirect(offsets[:, g * cols : (g + 1) * cols]))
            return picked

        bf0, dst = cast_views(0)
        nc.scalar.copy(out=dst, in_=raw_view(lc_raw0))
        th_raw = keep.tile([P, PACK, V], F32, name="th_raw", tag="lc0_th")
        nc.sync.dma_start(out=th_raw[:], in_=th.rearrange("(p j) w -> p j w", j=PACK))
        halves = [quantise_half(0, bf0)]

        alpha_t = bank(6, [P, 2, WH])
        nc.tensor.transpose(alpha_t[:, 0, 0:P], alpha_rows[:], ident[:])
        alpha_sb = keep.tile([P, TILES], F32, name="alpha_sb")
        nc.scalar.activation(out=alpha_sb[:], in_=alpha_t[:, 0, P - TILES : P], func=ACT.Copy, scale=-2.0)

        x_picked = [gather_words(g) for g in range(TILES // 2)]
        bf1, dst = cast_views(1)
        nc.scalar.copy(out=dst[:, 0:VQ], in_=raw_view(lc_raw1[0]))
        nc.scalar.activation(
            out=bf1[:].rearrange("p d v j -> p v d j")[:, VQ : VQ + HOLD_ARMS],
            in_=lc_raw1[1][:].rearrange("p j (v d) -> p v d j", d=D)[:, 0:HOLD_ARMS], func=ACT.Copy, scale=unit[:],
        )
        nc.scalar.copy(out=dst[:, VQ + HOLD_ARMS : VH], in_=raw_view(lc_raw1[1])[:, HOLD_ARMS:VQ])
        halves.append(quantise_half(1, bf1))

        def x_tile(t):
            g, i = divmod(t, 2)
            return x_picked[g][:, i * P : (i + 1) * P].bitcast(FP8X4), x_plane[:, t * P : (t + 1) * P]

        sq_a = [
            keep.tile([P, DIRECT, WH], F32, name="sq_a0", tag="unit_sq0"),
            keep.tile([P, 2, WH], F32, name="sq_a1"),
        ]

        def direct_products(h, b, lo, hi):
            codes, plane = halves[h]
            z = bank(b, [P, hi - lo, WH])
            for t in range(lo, hi):
                x_codes, x_scale = x_tile(t)
                nc.tensor.matmul_mx(
                    out=z[:, t - lo, :], lhsT=x_codes, lhsT_scale=x_scale,
                    rhs=codes[:].bitcast(FP8X4), rhs_scale=plane[:], start=True, stop=True,
                )
            return z

        for h, b, lo, hi in ((0, 7, 0, 1), (0, 0, 1, 2), (0, 1, 2, 4), (1, 2, 0, 2)):
            nc.scalar.activation(out=sq_a[h][:, lo:hi, :], in_=direct_products(h, b, lo, hi)[:], func=ACT.Square)

        th_bf = placed.tile([P, V, PACK], BF16, name="th_bf", offset=T // 2, align_bytes=64)
        nc.vector.tensor_scalar(
            out=th_bf[:].rearrange("p (c i) j -> p c j i", i=4), in0=th_raw[:].rearrange("p j (c i) -> p c j i", i=4),
            scalar1=-2.0, scalar2=None, op0=ALU.mult,
        )
        partial = keep.tile([P, 2, DIRECT, 2 * VH], F32, name="pair", tag="words_pair", align_bytes=64)
        sums_a = keep.tile([P, DIRECT, 2, VH], F32, name="sums_a")

        def add_first(g, h, sq):
            t = slice(2 * g, 2 * g + 2)
            nc.vector.tensor_tensor(
                out=partial[:, h, t, :], in0=sq[:, :, 0 : 2 * VH], in1=sq[:, :, 2 * VH : 4 * VH], op=ALU.add
            )

        def add_second(g):
            t = slice(2 * g, 2 * g + 2)
            nc.vector.tensor_tensor(
                out=sums_a[:, t].rearrange("p t h v -> p h t v"), in0=partial[:, :, t, 0:VH],
                in1=partial[:, :, t, VH : 2 * VH], op=ALU.add,
            )

        th_codes = keep.tile([P, V], U32, name="th_codes", align_bytes=64)
        th_plane = keep.tile([P, V], U8, name="th_plane", align_bytes=64)
        nc.vector.quantize_mx(
            out=th_codes[:].bitcast(FP8X4), scales=th_plane[:], in_=th_bf[:].rearrange("p v j -> p (v j)")
        )
        sq_b = {}

        def transposed_products(b, g, ds):
            z = bank(b, [P, len(ds), PAIR])
            for j, d in enumerate(ds):
                nc.tensor.matmul_mx(
                    out=z[:, j, :], lhsT=by_d_codes[:, d].rearrange("p h v -> p (h v)").bitcast(FP8X4),
                    lhsT_scale=by_d_plane[:, d].rearrange("p h v -> p (h v)"),
                    rhs=x_picked[g][:].bitcast(FP8X4),
                    rhs_scale=x_plane[:, g * PAIR : (g + 1) * PAIR], start=True, stop=True,
                )
            sq = keep.tile([P, len(ds), PAIR], F32, name=f"sq_b{g - 2}{ds[0]}")
            for j, d in enumerate(ds):
                sq_b[g, d] = sq[:, j, :]
            return z, sq

        def transposed_squares(b, g, ds):
            z, sq = transposed_products(b, g, ds)
            nc.scalar.activation(out=sq[:], in_=z[:], func=ACT.Square, bias=0.0)

        def products_with_th(n, b):
            y = bank(b, [P, DIRECT, V])
            for i in range(DIRECT):
                x_codes, x_scale = x_tile(n * DIRECT + i)
                nc.tensor.matmul_mx(
                    out=y[:, i, :], lhsT=x_codes, lhsT_scale=x_scale, rhs=th_codes[:].bitcast(FP8X4),
                    rhs_scale=th_plane[:], start=True, stop=True,
                )
            return y

        transposed_squares(4, 2, (0, 1))
        z_last = direct_products(1, 3, 2, 4)
        z_sb = keep.tile([P, 2, WH], F32, name="z_sb")
        sq_last = keep.tile([P, 2, WH], F32, name="sq_last")
        nc.vector.tensor_copy(out=z_sb[:], in_=z_last[:])
        add_first(0, 0, sq_a[0][:, 0:2, :])
        nc.vector.tensor_tensor(out=sq_last[:], in0=z_last[:], in1=z_sb[:], op=ALU.mult)
        add_first(0, 1, sq_a[1][:])
        add_first(1, 0, sq_a[0][:, 2:4, :])
        transposed_squares(5, 2, (2, 3))
        transposed_squares(6, 3, (0, 1))
        ys = [products_with_th(0, 7)]
        z, sq = transposed_products(4, 3, (2, 3))
        nc.scalar.activation(out=sq[:, 0, :], in_=z[:, 0, :], func=ACT.Square, bias=zero_late[:])
        nc.scalar.activation(out=sq[:, 1, :], in_=z[:, 1, :], func=ACT.Square)
        add_second(0)
        add_first(1, 1, sq_last[:])
        add_second(1)
        sums_v = sums_a[:].rearrange("p t h v -> p t (h v)")

        sums_b = {g: bank(g - 1, [P, 2, V]) for g in (2, 3)}
        for g in (2, 3):
            for d in range(D):
                for i in range(2):
                    nc.tensor.matmul(
                        out=sums_b[g][:, i, :], lhsT=sq_b[g, d][:, i * P : (i + 1) * P], rhs=ident[:],
                        is_transpose=True, start=(d == 0 and i == 0), stop=(d == D - 1 and i == 1),
                    )

        ys.append(products_with_th(1, 4))
        bon = keep.tile([P, TILES, V], F32, name="bon", tag="zero_bon_late_inv")
        sums = (sums_v[:, 0:2, :], sums_v[:, 2:4, :], sums_b[2][:], sums_b[3][:])
        order = (0, 2, 3, 1)
        for g in order:
            nc.scalar.activation(out=bon[:, 2 * g : 2 * g + 2, :], in_=sums[g], func=ACT.Sqrt, bias=floor[:])

        neg = keep.tile([P, TILES, V], F32, name="neg")
        bias = keep.tile([P, TILES], F32, name="bias", tag="floor_bias")

        def score(g):
            for t in (2 * g, 2 * g + 1):
                n, i = divmod(t, DIRECT)
                nc.vector.scalar_tensor_tensor(
                    out=neg[:, t, :], in0=bon[:, t, :], scalar=alpha_sb[:, t : t + 1], in1=ys[n][:, i, :],
                    op0=ALU.mult, op1=ALU.add,
                )

        def least(g):
            t = slice(2 * g, 2 * g + 2)
            nc.vector.tensor_reduce(out=bias[:, t], in_=neg[:, t, :], axis=AX.X, op=ALU.min)

        for g in order:
            score(g)
        for g in range(TILES // 2):
            least(g)

        ex = keep.tile([P, TILES, V], F32, name="ex")
        inv = keep.tile([P, TILES], F32, name="inv", tag="zero_bon_late_inv")
        res = keep.tile([P, TILES, V], F32, name="res")
        for t in range(TILES):
            total = keep.tile([P, 1], F32, name=f"total{t}")
            nc.scalar.activation(
                out=ex[:, t, :], in_=neg[:, t, :], func=ACT.Exp, bias=bias[:, t : t + 1], scale=-1.0,
                accum_out=total[:],
            )
            nc.vector.reciprocal(out=inv[:, t : t + 1], in_=total[:])
            if t > 0:
                u = t - 1
                nc.vector.tensor_scalar(
                    out=res[:, u, :], in0=ex[:, u, :], scalar1=inv[:, u : u + 1], scalar2=None, op0=ALU.mult
                )
        last = TILES - 1
        nc.scalar.activation(out=res[:, last, :], in_=ex[:, last, :], func=ACT.Copy, scale=inv[:, last : last + 1])

        out_v = out.rearrange("(i p) v -> p i v", p=P)
        for lo, hi in ((0, 3), (3, 6), (6, 7), (7, 8)):
            nc.sync.dma_start(out=out_v[:, lo:hi, :], in_=res[:, lo:hi, :])
